import numpy as np
import ml_dtypes


def mxq(x, axis, fmt="e4m3"):
    dtype, down = {"e4m3": (ml_dtypes.float8_e4m3fn, 7), "e5m2": (ml_dtypes.float8_e5m2, 14)}[fmt]
    v = np.moveaxis(np.asarray(x, np.float32).astype(ml_dtypes.bfloat16).astype(np.float64), axis, -1)
    blocks = v.reshape(v.shape[:-1] + (-1, 32))
    amax = np.abs(blocks).max(-1, keepdims=True)
    byte = np.maximum(np.where(amax > 0, np.frexp(amax)[1] - 1 + 127, 0) - down, 1)
    scale = np.exp2(byte - 127.0)
    codes = (blocks / scale).astype(np.float32).astype(dtype).astype(np.float64)
    return np.moveaxis((codes * scale).reshape(v.shape), -1, axis)


WIDE = False


def mx_kscale(k):
    if not WIDE:
        return np.ones(k)
    levels = np.array([24, -24, 12, -12, 0])
    if k % 512:
        return np.exp2(np.random.permutation(np.resize(levels, k // 32))).repeat(32)
    a = np.empty((k // 512, 16))
    for p in range(k // 512):
        a[p, :8] = np.random.permutation(np.resize(levels, 8))
        for g in range(8):
            far = levels[np.abs(levels - a[p, g]) >= 10]
            a[p, g + 8] = far[np.random.randint(len(far))]
    return np.exp2(a.ravel()).repeat(32)


def f64(x):
    return np.asarray(x).astype(np.float64)


def striped(idx):
    return np.tile(idx.reshape(-1, 16).T, (8, 1)).astype(np.uint16)


def unstriped(offs):
    return offs[:16].T.reshape(-1).astype(np.int64)


E2M1 = np.array([0.0, 0.5, 1.0, 1.5, 2.0, 3.0, 4.0, 6.0, -0.0, -0.5, -1.0, -1.5, -2.0, -3.0, -4.0, -6.0])


def pack_weight(w, fmt):
    k, n = w.shape
    w = f64(np.asarray(w, np.float32).astype(ml_dtypes.bfloat16)).reshape(k // 32, 32, n)
    amax = np.abs(w).max(1)
    if fmt == "e4m3":
        byte = np.frexp(amax)[1] - 1 + 127 - 7
    else:
        mant, ex = np.frexp(amax / 6.0)
        byte = np.where(mant > 0.5, ex, ex - 1) + 127
    byte = np.clip(np.where(amax > 0, byte, 1), 1, 254)
    scaled = (w * np.exp2(127.0 - byte)[:, None, :]).reshape(k, n).astype(np.float32)
    by_word = np.ascontiguousarray(scaled.reshape(k // 512, 128, 4, n).transpose(0, 1, 3, 2))
    if fmt == "e4m3":
        words = by_word.astype(ml_dtypes.float8_e4m3fn).view(np.uint8)
    else:
        c = by_word.astype(ml_dtypes.float4_e2m1fn).view(np.uint8) & 0xF
        words = (c[..., 0::2] | (c[..., 1::2] << 4)).reshape(k // 512, 128, 2 * n)
    return np.ascontiguousarray(words), np.ascontiguousarray(byte.astype(np.uint8).reshape(k // 512, 16, n))


def unpack_weight(words, scales, fmt):
    g, _, n = scales.shape
    words = np.ascontiguousarray(words).reshape(g, 128, n, -1)
    if fmt == "e4m3":
        vals = words.view(ml_dtypes.float8_e4m3fn).astype(np.float64)
    else:
        nib = np.empty((g, 128, n, 4), np.uint8)
        nib[..., 0::2] = words & 0xF
        nib[..., 1::2] = words >> 4
        vals = E2M1[nib]
    vals = vals * np.repeat(np.exp2(scales.astype(np.float64) - 127.0), 8, axis=1)[..., None]
    return vals.transpose(0, 1, 3, 2).reshape(g * 512, n)


def pack_table4(v):
    words, scales = pack_weight(v, "e2m1")
    g, t = words.shape[0] // 2, v.shape[1]
    return np.ascontiguousarray(words.reshape(g, 2, 128, t, 2).transpose(0, 2, 3, 1, 4).reshape(g, 128, t, 4)), scales


def unpack_table4(words, scales):
    g, _, t, _ = words.shape
    return unpack_weight(words.reshape(g, 128, t, 2, 2).transpose(0, 3, 1, 2, 4).reshape(2 * g, 128, 2 * t), scales, "e2m1")


def gelu(f):
    return 0.5 * f * (1.0 + np.tanh(np.sqrt(2.0 / np.pi) * (f + 0.044715 * f**3)))


K, R, N, T, J = 1024, 512, 512, 2048, 1024


def setup_inputs():
    n = np.random.standard_normal
    s = mx_kscale(K)[:, None]
    u = mx_kscale(R)[:, None]
    p_tab = pack_table4(n((K, T)) * s)
    p_wt = pack_weight(n((K, R)) / np.sqrt(2 * K) / s, "e4m3")
    return {
        "tab_words": p_tab[0],
        "tab_scales": p_tab[1],
        "ws": (n((K, R)) / np.sqrt(2 * K) / s).astype(np.float32),
        "wt_words": p_wt[0],
        "wt_scales": p_wt[1],
        "sm": (np.random.uniform(0.5, 2.0, R) * u[:, 0]).astype(np.float32),
        "wd": (n((R, N)) / np.sqrt(R) / u).astype(np.float32),
        "gT": (n((N, T))).astype(np.float32),
        "wgo": np.tile(np.random.uniform(0.5, 2.0, J), (128, 1)).astype(np.float32),
        "offs": striped(np.random.permutation(T)[:J]),
        "offs2": striped(np.random.permutation(T)[:J]),
    }


def reference(tab_words, tab_scales, ws, wt_words, wt_scales, sm, wd, gT, wgo, offs, offs2):
    idx = unstriped(offs)
    idx2 = unstriped(offs2)
    tab_ = unpack_table4(tab_words, tab_scales)[:, idx]
    tabb_ = unpack_table4(tab_words, tab_scales)[:, idx2]
    ws_ = mxq(f64(ws), 0, "e4m3")
    wt_ = unpack_weight(wt_words, wt_scales, "e4m3")
    a = ws_.T @ tab_ + wt_.T @ tabb_
    h = f64(sm)[:, None] * gelu(a)
    h_ = mxq(h, 0, "e4m3")
    wd_ = mxq(f64(wd), 0, "e4m3")
    y = wd_.T @ h_
    out = np.zeros((N, T))
    out[:, idx2] = f64(wgo)[0] * (y * f64(gT)[:, idx])
    return out

@@ -1,0 +1,235 @@
+from contextlib import ExitStack
+
+import concourse.mybir as mybir
+
+K, R, N, T, J = 1024, 512, 512, 2048, 1024
+FLOPS = 2 * J * R * (2 * K + N)
+
+F32 = mybir.dt.float32
+BF16 = mybir.dt.bfloat16
+I32 = mybir.dt.int32
+U32 = mybir.dt.uint32
+U16 = mybir.dt.uint16
+U8 = mybir.dt.uint8
+FP8X4 = mybir.dt.float8_e4m3fn_x4
+FP4X4 = mybir.dt.float4_e2m1fn_x4
+MULT = mybir.AluOpType.mult
+ACT = mybir.ActivationFunctionType
+
+P = 128
+PACK = 4
+PASSES = K // (P * PACK)
+QUADS = 4
+HALF = 512
+HALVES = J // HALF
+COLS = HALF // 16
+RUN = 8
+GROUPS = R // (PACK * RUN)
+PAGES = N // P
+
+
+def tile_list_msg_gelu_gate_kernel(
+    tc, tab_words, tab_scales, ws, wt_words, wt_scales, sm, wd, gT, wgo, offs, offs2, out
+):
+    nc = tc.nc
+    with ExitStack() as ctx:
+        keep = ctx.enter_context(tc.tile_pool(name="keep", bufs=1))
+        psum = ctx.enter_context(tc.psum_pool(name="psum", bufs=1))
+
+        def sb(name, shape, dtype, tag=None):
+            return keep.tile(shape, dtype, name=name, tag=tag or name, align_bytes=64)
+
+        lists = [keep.tile([P, J // 16], U16, name="src_list"), keep.tile([P, J // 16], U16, name="dst_list")]
+        tab_sc = sb("tab_sc", [P, T], U8)
+        wt_sc_raw = sb("wt_sc_raw", [P, PASSES * R], U8)
+        tab_planes = sb("tab_planes", [P, PASSES * 2 * J], U8)
+        pages = [sb("page0", [P, T], F32), sb("page1", [P, T], F32)]
+
+        nc.vector.memset(tab_sc[0:96, :].bitcast(I32), 0)
+        nc.vector.memset(wt_sc_raw[:].bitcast(I32), 0)
+        for page in pages:
+            nc.vector.memset(page[:], 0.0)
+
+        sm_sb = [sb("sm_sb%d" % t, [P, 1], F32) for t in range(PACK)]
+        sm_rows = sm.rearrange("(g t i) -> t g i", t=PACK, i=RUN)
+        with nc.allow_non_contiguous_dma(reason="one smoothing factor a partition"):
+            for t in range(PACK):
+                nc.gpsimd.dma_start(sm_sb[t][:], sm_rows[t].unsqueeze(2))
+        nc.gpsimd.memset(tab_planes[:].bitcast(I32), 0)
+        for n in range(2, PAGES):
+            page = sb("page%d" % n, [P, T], F32)
+            for c in range(2):
+                nc.gpsimd.memset(page[:, c * J : (c + 1) * J], 0.0)
+            pages.append(page)
+
+        nc.sync.dma_start(lists[0][:], offs)
+        nc.sync.dma_start(tab_sc[96:P, :].bitcast(I32), tab_scales.rearrange("a q t -> q a t").bitcast(I32))
+        nc.sync.dma_start(lists[1][:], offs2)
+
+        ws_raw = [sb("ws_raw%d" % a, [P, PACK, R], F32) for a in range(PASSES)]
+        ws_rows = ws.rearrange("(a p i) r -> a p i r", a=PASSES, i=PACK)
+        nc.sync.dma_start(ws_raw[0][:], ws_rows[0])
+        tab_w = sb("tab_w", [P, T], I32)
+        nc.sync.dma_start(tab_w[:], tab_words[0].rearrange("p t b -> p (t b)").bitcast(I32))
+        wt_raw = sb("wt_raw", [P, PASSES, R], I32)
+        nc.sync.dma_start(wt_raw[:], wt_words.rearrange("a p r b -> p a (r b)").bitcast(I32))
+        for q in range(QUADS):
+            nc.scalar.dma_start(
+                wt_sc_raw[32 * q : 32 * q + 4, :].bitcast(I32).rearrange("p (a r) -> p a r", a=PASSES),
+                wt_scales[:, 4 * q : 4 * q + 4, :].bitcast(I32).rearrange("a p r -> p a r"),
+            )
+        nc.sync.dma_start(ws_raw[1][:], ws_rows[1])
+
+        picked_sc = sb("picked_sc", [P, 2 * J], U8)
+        for side in range(2):
+            nc.vector.tensor_copy(picked_sc[:, side * J : (side + 1) * J], tab_sc[:].indirect(lists[side][:]))
+        for q in range(QUADS):
+            nc.sync.dma_start(
+                tab_planes[32 * q : 32 * q + 4, :].bitcast(I32).rearrange("p (a j) -> p a j", a=PASSES),
+                picked_sc[96 + 8 * q : 96 + 8 * q + 8, :].bitcast(I32),
+            )
+
+        wd_raw = sb("wd_raw", [P, PACK, N], F32)
+        wd_rows = wd.rearrange("(g t i) n -> t g i n", t=PACK, i=RUN)
+        for t in range(PACK):
+            nc.sync.dma_start(wd_raw[:, t, :], wd_rows[t])
+        ws_codes, ws_sc = [], []
+
+        def round_ws(a):
+            grouped = sb("ws_bf%d" % a, [P, R * PACK], BF16)
+            nc.scalar.copy(
+                grouped[:].rearrange("p (t g m i) -> p t g m i", t=PACK, g=GROUPS, m=RUN),
+                ws_raw[a][:].rearrange("p i (g t m) -> p t g m i", t=PACK, m=RUN),
+            )
+            return grouped
+
+        def quantise(name, grouped, width):
+            codes = sb(name + "_codes", [P, width], U32)
+            scales = sb(name + "_sc", [P, width], U8)
+            nc.vector.quantize_mx(out=codes[:].bitcast(FP8X4), scales=scales[:], in_=grouped[:])
+            return codes, scales
+
+        wt_codes = sb("wt_codes", [P, PASSES, R], I32)
+        wt_sc = sb("wt_sc", [P, PASSES * R], U8)
+        for a in range(PASSES):
+            nc.gpsimd.tensor_copy(
+                wt_codes[:, a, :].rearrange("p (t g m) -> p t g m", t=PACK, m=RUN),
+                wt_raw[:, a, :].rearrange("p (g t m) -> p t g m", t=PACK, m=RUN),
+            )
+        nc.gpsimd.tensor_copy(
+            wt_sc[:].bitcast(I32).rearrange("p (a t g m) -> p a t g m", a=PASSES, t=PACK, g=GROUPS),
+            wt_sc_raw[:].bitcast(I32).rearrange("p (a g t m) -> p a t g m", a=PASSES, t=PACK, g=GROUPS),
+        )
+
+        def pick_words(h, tag):
+            picked = sb("picked_w%d" % h, [P, 2 * HALF], U32, tag=tag)
+            for side in range(2):
+                nc.vector.tensor_copy(
+                    picked[:, side * HALF : (side + 1) * HALF],
+                    tab_w[:].bitcast(U32).indirect(lists[side][:, h * COLS : (h + 1) * COLS]),
+                )
+            return picked
+
+        def part_words(h, picked, tag):
+            parted = sb("parted%d" % h, [P, 2 * PASSES * HALF * 2], U8, tag=tag)
+            for side in range(2):
+                nc.vector.tensor_copy(
+                    parted[:, side * 4 * HALF : (side + 1) * 4 * HALF].bitcast(U16).rearrange("p (a j) -> p a j", a=PASSES),
+                    picked[:, side * HALF : (side + 1) * HALF].bitcast(U16).rearrange("p (j a) -> p a j", a=PASSES),
+                )
+            return parted
+
+        ws_bf = [round_ws(a) for a in range(PASSES)]
+        parted = [part_words(0, pick_words(0, None), None)]
+        ws_q = [quantise("ws0", ws_bf[0], R)]
+        picked = pick_words(1, "ws_bf0")
+        ws_q.append(quantise("ws1", ws_bf[1], R))
+        parted.append(part_words(1, picked, "ws_bf1"))
+
+        wgo_sb = sb("wgo_sb", [P, J], F32, tag="tab_sc")
+        nc.sync.dma_start(wgo_sb[:], wgo)
+        gates = []
+        for n, tag in enumerate(("ws_raw0", "wt_raw", "ws_raw1", "tab_w")):
+            gates.append(sb("gates%d" % n, [P, T], F32, tag=tag))
+            nc.sync.dma_start(gates[n][:], gT[n * P : (n + 1) * P, :])
+
+        wd_bf = sb("wd_bf", [P, N * PACK], BF16)
+        nc.scalar.copy(wd_bf[:].rearrange("p (n t) -> p n t", t=PACK), wd_raw[:].rearrange("p t n -> p n t"))
+        wd_codes, wd_sc = quantise("wd", wd_bf, N)
+
+        def first_product(h):
+            banks = [psum.tile([P, HALF], F32, name="a%d%d" % (h, t), tag="bank%d" % (PACK * h + t)) for t in range(PACK)]
+            order = [(0, 0), (1, 0), (1, 1), (0, 1)]
+            for t in range(PACK):
+                cols = slice(t * P, (t + 1) * P)
+                for step, (side, a) in enumerate(order):
+                    if side == 0:
+                        w_codes, w_sc = ws_q[a][0][:, cols], ws_q[a][1][:, cols]
+                    else:
+                        w_codes = wt_codes[:, a, cols]
+                        w_sc = wt_sc[:, a * R + t * P : a * R + (t + 1) * P]
+                    nc.tensor.matmul_mx(
+                        out=banks[t][:],
+                        lhsT=w_codes.bitcast(FP8X4),
+                        lhsT_scale=w_sc,
+                        rhs=parted[h][:, (2 * side + a) * 2 * HALF : (2 * side + a + 1) * 2 * HALF].bitcast(FP4X4),
+                        rhs_scale=tab_planes[:, (2 * a + side) * J + h * HALF : (2 * a + side) * J + (h + 1) * HALF],
+                        start=(step == 0),
+                        stop=(step == len(order) - 1),
+                    )
+            return banks
+
+        def hidden(h, banks):
+            act = sb("act%d" % h, [P, PACK, HALF], F32)
+            rounded = sb("rounded%d" % h, [P, PACK, HALF], BF16)
+            for t in range(PACK):
+                nc.scalar.activation(act[:, t, :], banks[t][:], ACT.Gelu_apprx_tanh)
+            for t in range(PACK):
+                nc.scalar.activation(rounded[:, t, :], act[:, t, :], ACT.Copy, scale=sm_sb[t][:])
+            grouped = sb("h_bf%d" % h, [P, HALF * PACK], BF16)
+            nc.scalar.copy(grouped[:].rearrange("p (j t) -> p j t", t=PACK), rounded[:].rearrange("p t j -> p j t"))
+            return grouped
+
+        def second_product(h, h_codes, h_sc):
+            msgs = []
+            for n in range(PAGES):
+                bank = psum.tile([P, HALF], F32, name="y%d%d" % (h, n), tag="bank%d" % (PACK * h + n))
+                nc.tensor.matmul_mx(
+                    out=bank[:],
+                    lhsT=wd_codes[:, n * P : (n + 1) * P].bitcast(FP8X4),
+                    lhsT_scale=wd_sc[:, n * P : (n + 1) * P],
+                    rhs=h_codes[:].bitcast(FP8X4),
+                    rhs_scale=h_sc[:],
+                    start=True,
+                    stop=True,
+                )
+                msg = sb("msg%d%d" % (h, n), [P, HALF], F32)
+                nc.scalar.copy(msg[:], bank[:])
+                msgs.append(msg)
+            return msgs
+
+        sums = [first_product(h) for h in range(HALVES)]
+
+        def weigh_gates(h, pair, tag):
+            both = sb("gate_w%d%d" % (h, pair), [P, 2 * HALF], F32, tag=tag)
+            for c in range(2):
+                nc.vector.tensor_tensor(
+                    both[:, c * HALF : (c + 1) * HALF],
+                    gates[2 * pair + c][:].indirect(lists[0][:, h * COLS : (h + 1) * COLS]),
+                    wgo_sb[:, h * HALF : (h + 1) * HALF],
+                    MULT,
+                )
+            return [both[:, c * HALF : (c + 1) * HALF] for c in range(2)]
+
+        weighted = [weigh_gates(0, 0, None) + weigh_gates(0, 1, None), []]
+
+        for h in range(HALVES):
+            h_codes, h_sc = quantise("h%d" % h, hidden(h, sums[h]), HALF)
+            weighted[1].extend(weigh_gates(1, h, "h_bf%d" % h))
+            msgs = second_product(h, h_codes, h_sc)
+            for n in range(PAGES):
+                nc.vector.tensor_tensor(
+                    pages[n][:].indirect(lists[1][:, h * COLS : (h + 1) * COLS]), msgs[n][:], weighted[h][n], MULT
+                )
+        for n in range(PAGES):
+            nc.sync.dma_start(out[n * P : (n + 1) * P, :], pages[n][:])

@@ -47,15 +47,16 @@ def tile_list_msg_gelu_gate_kernel(
 
         nc.vector.memset(tab_sc[0:96, :].bitcast(I32), 0)
         nc.vector.memset(wt_sc_raw[:].bitcast(I32), 0)
-        for page in pages:
-            nc.vector.memset(page[:], 0.0)
+        nc.vector.memset(tab_planes[:].bitcast(I32), 0)
+        nc.vector.memset(pages[0][:], 0.0)
+        nc.vector.memset(pages[1][:, 0:J], 0.0)
 
         sm_sb = [sb("sm_sb%d" % t, [P, 1], F32) for t in range(PACK)]
         sm_rows = sm.rearrange("(g t i) -> t g i", t=PACK, i=RUN)
         with nc.allow_non_contiguous_dma(reason="one smoothing factor a partition"):
             for t in range(PACK):
                 nc.gpsimd.dma_start(sm_sb[t][:], sm_rows[t].unsqueeze(2))
-        nc.gpsimd.memset(tab_planes[:].bitcast(I32), 0)
+        nc.gpsimd.memset(pages[1][:, J:T], 0.0)
         for n in range(2, PAGES):
             page = sb("page%d" % n, [P, T], F32)
             for c in range(2):
@@ -71,6 +72,7 @@ def tile_list_msg_gelu_gate_kernel(
         nc.sync.dma_start(ws_raw[0][:], ws_rows[0])
         tab_w = sb("tab_w", [P, T], I32)
         nc.sync.dma_start(tab_w[:], tab_words[0].rearrange("p t b -> p (t b)").bitcast(I32))
+        nc.sync.dma_start(ws_raw[1][:], ws_rows[1])
         wt_raw = sb("wt_raw", [P, PASSES, R], I32)
         nc.sync.dma_start(wt_raw[:], wt_words.rearrange("a p r b -> p a (r b)").bitcast(I32))
         for q in range(QUADS):
@@ -78,7 +80,6 @@ def tile_list_msg_gelu_gate_kernel(
                 wt_sc_raw[32 * q : 32 * q + 4, :].bitcast(I32).rearrange("p (a r) -> p a r", a=PASSES),
                 wt_scales[:, 4 * q : 4 * q + 4, :].bitcast(I32).rearrange("a p r -> p a r"),
             )
-        nc.sync.dma_start(ws_raw[1][:], ws_rows[1])
 
         picked_sc = sb("picked_sc", [P, 2 * J], U8)
         for side in range(2):
@@ -89,7 +90,7 @@ def tile_list_msg_gelu_gate_kernel(
                 picked_sc[96 + 8 * q : 96 + 8 * q + 8, :].bitcast(I32),
             )
 
-        wd_raw = sb("wd_raw", [P, PACK, N], F32)
+        wd_raw = sb("wd_raw", [P, PACK, N], F32, tag="tab_sc")
         wd_rows = wd.rearrange("(g t i) n -> t g i n", t=PACK, i=RUN)
         for t in range(PACK):
             nc.sync.dma_start(wd_raw[:, t, :], wd_rows[t])
@@ -108,18 +109,6 @@ def tile_list_msg_gelu_gate_kernel(
             scales = sb(name + "_sc", [P, width], U8)
             nc.vector.quantize_mx(out=codes[:].bitcast(FP8X4), scales=scales[:], in_=grouped[:])
             return codes, scales
-
-        wt_codes = sb("wt_codes", [P, PASSES, R], I32)
-        wt_sc = sb("wt_sc", [P, PASSES * R], U8)
-        for a in range(PASSES):
-            nc.gpsimd.tensor_copy(
-                wt_codes[:, a, :].rearrange("p (t g m) -> p t g m", t=PACK, m=RUN),
-                wt_raw[:, a, :].rearrange("p (g t m) -> p t g m", t=PACK, m=RUN),
-            )
-        nc.gpsimd.tensor_copy(
-            wt_sc[:].bitcast(I32).rearrange("p (a t g m) -> p a t g m", a=PASSES, t=PACK, g=GROUPS),
-            wt_sc_raw[:].bitcast(I32).rearrange("p (a g t m) -> p a t g m", a=PASSES, t=PACK, g=GROUPS),
-        )
 
         def pick_words(h, tag):
             picked = sb("picked_w%d" % h, [P, 2 * HALF], U32, tag=tag)
@@ -142,14 +131,25 @@ def tile_list_msg_gelu_gate_kernel(
         ws_bf = [round_ws(a) for a in range(PASSES)]
         parted = [part_words(0, pick_words(0, None), None)]
         ws_q = [quantise("ws0", ws_bf[0], R)]
-        picked = pick_words(1, "ws_bf0")
-        ws_q.append(quantise("ws1", ws_bf[1], R))
-        parted.append(part_words(1, picked, "ws_bf1"))
+        wt_codes = sb("wt_codes", [P, PASSES, R], I32, tag="ws_bf0")
+        wt_sc = sb("wt_sc", [P, PASSES * R], U8, tag="picked_w0")
+        for a in range(PASSES):
+            nc.vector.tensor_copy(
+                wt_codes[:, a, :].rearrange("p (t g m) -> p t g m", t=PACK, m=RUN),
+                wt_raw[:, a, :].rearrange("p (g t m) -> p t g m", t=PACK, m=RUN),
+            )
+        nc.vector.tensor_copy(
+            wt_sc[:].bitcast(I32).rearrange("p (a t g m) -> p a t g m", a=PASSES, t=PACK, g=GROUPS),
+            wt_sc_raw[:].bitcast(I32).rearrange("p (a g t m) -> p a t g m", a=PASSES, t=PACK, g=GROUPS),
+        )
 
-        wgo_sb = sb("wgo_sb", [P, J], F32, tag="tab_sc")
+        ws_q.append(quantise("ws1", ws_bf[1], R))
+        parted.append(part_words(1, pick_words(1, "ws_bf1"), None))
+
+        wgo_sb = sb("wgo_sb", [P, J], F32, tag="ws_raw0")
         nc.sync.dma_start(wgo_sb[:], wgo)
         gates = []
-        for n, tag in enumerate(("ws_raw0", "wt_raw", "ws_raw1", "tab_w")):
+        for n, tag in enumerate(("wt_raw", "wt_sc_raw", "ws_raw1", "tab_w")):
             gates.append(sb("gates%d" % n, [P, T], F32, tag=tag))
             nc.sync.dma_start(gates[n][:], gT[n * P : (n + 1) * P, :])
 
@@ -159,7 +159,7 @@ def tile_list_msg_gelu_gate_kernel(
 
         def first_product(h):
             banks = [psum.tile([P, HALF], F32, name="a%d%d" % (h, t), tag="bank%d" % (PACK * h + t)) for t in range(PACK)]
-            order = [(0, 0), (1, 0), (1, 1), (0, 1)]
+            order = [(1, 0), (1, 1), (0, 0), (0, 1)]
             for t in range(PACK):
                 cols = slice(t * P, (t + 1) * P)
                 for step, (side, a) in enumerate(order):
@@ -210,26 +210,33 @@ def tile_list_msg_gelu_gate_kernel(
 
         sums = [first_product(h) for h in range(HALVES)]
 
-        def weigh_gates(h, pair, tag):
-            both = sb("gate_w%d%d" % (h, pair), [P, 2 * HALF], F32, tag=tag)
-            for c in range(2):
+        weighted = {}
+
+        def weigh_gates(name, parts, tag):
+            held = sb(name, [P, len(parts) * HALF], F32, tag=tag)
+            for c, (h, n) in enumerate(parts):
+                weighted[h, n] = held[:, c * HALF : (c + 1) * HALF]
                 nc.vector.tensor_tensor(
-                    both[:, c * HALF : (c + 1) * HALF],
-                    gates[2 * pair + c][:].indirect(lists[0][:, h * COLS : (h + 1) * COLS]),
+                    weighted[h, n],
+                    gates[n][:].indirect(lists[0][:, h * COLS : (h + 1) * COLS]),
                     wgo_sb[:, h * HALF : (h + 1) * HALF],
                     MULT,
                 )
-            return [both[:, c * HALF : (c + 1) * HALF] for c in range(2)]
 
-        weighted = [weigh_gates(0, 0, None) + weigh_gates(0, 1, None), []]
+        def place(h, n, msg):
+            nc.vector.tensor_tensor(pages[n][:].indirect(lists[1][:, h * COLS : (h + 1) * COLS]), msg[:], weighted[h, n], MULT)
 
-        for h in range(HALVES):
-            h_codes, h_sc = quantise("h%d" % h, hidden(h, sums[h]), HALF)
-            weighted[1].extend(weigh_gates(1, h, "h_bf%d" % h))
-            msgs = second_product(h, h_codes, h_sc)
-            for n in range(PAGES):
-                nc.vector.tensor_tensor(
-                    pages[n][:].indirect(lists[1][:, h * COLS : (h + 1) * COLS]), msgs[n][:], weighted[h][n], MULT
-                )
+        weigh_gates("gate_w_early", [(0, 0), (1, 0), (0, 1), (1, 1), (0, 2)], None)
+        h_codes, h_sc = quantise("h0", hidden(0, sums[0]), HALF)
+        weigh_gates("gate_w_mid", [(1, 2), (1, 3)], "h_bf0")
+        msgs = [second_product(0, h_codes, h_sc)]
+        for n in range(PAGES - 1):
+            place(0, n, msgs[0][n])
+        h_codes, h_sc = quantise("h1", hidden(1, sums[1]), HALF)
+        weigh_gates("gate_w_late", [(0, 3)], "h_bf1")
+        msgs.append(second_product(1, h_codes, h_sc))
+        place(0, PAGES - 1, msgs[0][PAGES - 1])
+        for n in range(PAGES):
+            place(1, n, msgs[1][n])
         for n in range(PAGES):
             nc.sync.dma_start(out[n * P : (n + 1) * P, :], pages[n][:])

@@ -43,25 +43,18 @@ def tile_list_msg_gelu_gate_kernel(
         tab_sc = sb("tab_sc", [P, T], U8)
         wt_sc_raw = sb("wt_sc_raw", [P, PASSES * R], U8)
         tab_planes = sb("tab_planes", [P, PASSES * 2 * J], U8)
-        pages = [sb("page0", [P, T], F32), sb("page1", [P, T], F32)]
+        pages = [sb("page0", [P, T], F32)]
 
         nc.vector.memset(tab_sc[0:96, :].bitcast(I32), 0)
         nc.vector.memset(wt_sc_raw[:].bitcast(I32), 0)
         nc.vector.memset(tab_planes[:].bitcast(I32), 0)
         nc.vector.memset(pages[0][:], 0.0)
-        nc.vector.memset(pages[1][:, 0:J], 0.0)
 
         sm_sb = [sb("sm_sb%d" % t, [P, 1], F32) for t in range(PACK)]
         sm_rows = sm.rearrange("(g t i) -> t g i", t=PACK, i=RUN)
         with nc.allow_non_contiguous_dma(reason="one smoothing factor a partition"):
             for t in range(PACK):
                 nc.gpsimd.dma_start(sm_sb[t][:], sm_rows[t].unsqueeze(2))
-        nc.gpsimd.memset(pages[1][:, J:T], 0.0)
-        for n in range(2, PAGES):
-            page = sb("page%d" % n, [P, T], F32)
-            for c in range(2):
-                nc.gpsimd.memset(page[:, c * J : (c + 1) * J], 0.0)
-            pages.append(page)
 
         nc.sync.dma_start(lists[0][:], offs)
         nc.sync.dma_start(tab_sc[96:P, :].bitcast(I32), tab_scales.rearrange("a q t -> q a t").bitcast(I32))
@@ -157,6 +150,15 @@ def tile_list_msg_gelu_gate_kernel(
         nc.scalar.copy(wd_bf[:].rearrange("p (n t) -> p n t", t=PACK), wd_raw[:].rearrange("p t n -> p n t"))
         wd_codes, wd_sc = quantise("wd", wd_bf, N)
 
+        def clear_page(tag):
+            page = sb("page%d" % len(pages), [P, T], F32, tag=tag)
+            for c in range(2):
+                nc.gpsimd.memset(page[:, c * J : (c + 1) * J], 0.0)
+            pages.append(page)
+
+        clear_page("ws_bf1")
+        clear_page("wd_bf")
+
         def first_product(h):
             banks = [psum.tile([P, HALF], F32, name="a%d%d" % (h, t), tag="bank%d" % (PACK * h + t)) for t in range(PACK)]
             order = [(1, 0), (1, 1), (0, 0), (0, 1)]
@@ -229,6 +231,7 @@ def tile_list_msg_gelu_gate_kernel(
         weigh_gates("gate_w_early", [(0, 0), (1, 0), (0, 1), (1, 1), (0, 2)], None)
         h_codes, h_sc = quantise("h0", hidden(0, sums[0]), HALF)
         weigh_gates("gate_w_mid", [(1, 2), (1, 3)], "h_bf0")
+        clear_page("ws_raw1")
         msgs = [second_product(0, h_codes, h_sc)]
         for n in range(PAGES - 1):
             place(0, n, msgs[0][n])

@@ -34,24 +34,36 @@ def tile_list_msg_gelu_gate_kernel(
     nc = tc.nc
     with ExitStack() as ctx:
         keep = ctx.enter_context(tc.tile_pool(name="keep", bufs=1))
+        laid = ctx.enter_context(tc.tile_pool(name="laid", bufs=1))
         psum = ctx.enter_context(tc.psum_pool(name="psum", bufs=1))
 
         def sb(name, shape, dtype, tag=None):
             return keep.tile(shape, dtype, name=name, tag=tag or name, align_bytes=64)
 
+        def at(name, shape, dtype, offset):
+            return laid.tile(shape, dtype, name=name, tag=name, align_bytes=64, offset=offset)
+
         lists = [keep.tile([P, J // 16], U16, name="src_list"), keep.tile([P, J // 16], U16, name="dst_list")]
         tab_sc = sb("tab_sc", [P, T], U8)
         wt_sc_raw = sb("wt_sc_raw", [P, PASSES * R], U8)
         tab_planes = sb("tab_planes", [P, PASSES * 2 * J], U8)
-        pages = [sb("page0", [P, T], F32)]
+        pages = [sb("page%d" % n, [P, T], F32) for n in range(PAGES)]
 
         nc.vector.memset(tab_sc[0:96, :].bitcast(I32), 0)
-        nc.vector.memset(wt_sc_raw[:].bitcast(I32), 0)
         nc.vector.memset(tab_planes[:].bitcast(I32), 0)
         nc.vector.memset(pages[0][:], 0.0)
 
+        nc.gpsimd.memset(wt_sc_raw[:].bitcast(I32), 0)
+        for q in range(QUADS):
+            nc.gpsimd.dma_start(
+                wt_sc_raw[32 * q : 32 * q + 4, :].bitcast(I32).rearrange("p (a r) -> p a r", a=PASSES),
+                wt_scales[:, 4 * q : 4 * q + 4, :].bitcast(I32).rearrange("a p r -> p a r"),
+            )
+        for n in range(1, PAGES):
+            for c in range(2):
+                nc.gpsimd.memset(pages[n][:, c * J : (c + 1) * J], 0.0)
         sm_sb = [sb("sm_sb%d" % t, [P, 1], F32) for t in range(PACK)]
-        sm_rows = sm.rearrange("(g t i) -> t g i", t=PACK, i=RUN)
+        sm_rows = sm.rearrange("(g t m) -> t g m", t=PACK, m=RUN)
         with nc.allow_non_contiguous_dma(reason="one smoothing factor a partition"):
             for t in range(PACK):
                 nc.gpsimd.dma_start(sm_sb[t][:], sm_rows[t].unsqueeze(2))
@@ -60,7 +72,7 @@ def tile_list_msg_gelu_gate_kernel(
         nc.sync.dma_start(tab_sc[96:P, :].bitcast(I32), tab_scales.rearrange("a q t -> q a t").bitcast(I32))
         nc.sync.dma_start(lists[1][:], offs2)
 
-        ws_raw = [sb("ws_raw%d" % a, [P, PACK, R], F32) for a in range(PASSES)]
+        ws_raw = [sb("ws_raw0", [P, PACK, R], F32), at("ws_raw1", [P, PACK, R], F32, 0)]
         ws_rows = ws.rearrange("(a p i) r -> a p i r", a=PASSES, i=PACK)
         nc.sync.dma_start(ws_raw[0][:], ws_rows[0])
         tab_w = sb("tab_w", [P, T], I32)
@@ -68,11 +80,6 @@ def tile_list_msg_gelu_gate_kernel(
         nc.sync.dma_start(ws_raw[1][:], ws_rows[1])
         wt_raw = sb("wt_raw", [P, PASSES, R], I32)
         nc.sync.dma_start(wt_raw[:], wt_words.rearrange("a p r b -> p a (r b)").bitcast(I32))
-        for q in range(QUADS):
-            nc.scalar.dma_start(
-                wt_sc_raw[32 * q : 32 * q + 4, :].bitcast(I32).rearrange("p (a r) -> p a r", a=PASSES),
-                wt_scales[:, 4 * q : 4 * q + 4, :].bitcast(I32).rearrange("a p r -> p a r"),
-            )
 
         picked_sc = sb("picked_sc", [P, 2 * J], U8)
         for side in range(2):
@@ -87,7 +94,6 @@ def tile_list_msg_gelu_gate_kernel(
         wd_rows = wd.rearrange("(g t i) n -> t g i n", t=PACK, i=RUN)
         for t in range(PACK):
             nc.sync.dma_start(wd_raw[:, t, :], wd_rows[t])
-        ws_codes, ws_sc = [], []
 
         def round_ws(a):
             grouped = sb("ws_bf%d" % a, [P, R * PACK], BF16)
@@ -103,68 +109,58 @@ def tile_list_msg_gelu_gate_kernel(
             nc.vector.quantize_mx(out=codes[:].bitcast(FP8X4), scales=scales[:], in_=grouped[:])
             return codes, scales
 
-        def pick_words(h, tag):
-            picked = sb("picked_w%d" % h, [P, 2 * HALF], U32, tag=tag)
+        def pick_words(h, picked):
             for side in range(2):
-                nc.vector.tensor_copy(
-                    picked[:, side * HALF : (side + 1) * HALF],
-                    tab_w[:].bitcast(U32).indirect(lists[side][:, h * COLS : (h + 1) * COLS]),
-                )
-            return picked
+                nc.vector.tensor_copy(picked[side][:], tab_w[:].bitcast(U32).indirect(lists[side][:, h * COLS : (h + 1) * COLS]))
 
-        def part_words(h, picked, tag):
-            parted = sb("parted%d" % h, [P, 2 * PASSES * HALF * 2], U8, tag=tag)
+        def part_words(h, picked):
+            parted = []
             for side in range(2):
+                parted.append(sb("parted%d%d" % (h, side), [P, PASSES * HALF * 2], U8))
                 nc.vector.tensor_copy(
-                    parted[:, side * 4 * HALF : (side + 1) * 4 * HALF].bitcast(U16).rearrange("p (a j) -> p a j", a=PASSES),
-                    picked[:, side * HALF : (side + 1) * HALF].bitcast(U16).rearrange("p (j a) -> p a j", a=PASSES),
+                    parted[side][:].bitcast(U16).rearrange("p (a j) -> p a j", a=PASSES),
+                    picked[side][:].bitcast(U16).rearrange("p (j a) -> p a j", a=PASSES),
                 )
             return parted
 
         ws_bf = [round_ws(a) for a in range(PASSES)]
-        parted = [part_words(0, pick_words(0, None), None)]
         ws_q = [quantise("ws0", ws_bf[0], R)]
-        wt_codes = sb("wt_codes", [P, PASSES, R], I32, tag="ws_bf0")
-        wt_sc = sb("wt_sc", [P, PASSES * R], U8, tag="picked_w0")
+        picked = [sb("picked_w0%d" % side, [P, HALF], U32) for side in range(2)]
+        pick_words(0, picked)
+        parted = [part_words(0, picked)]
+        wt_codes = sb("wt_codes", [P, PASSES, R], I32)
+        wt_sc = sb("wt_sc", [P, PASSES * R], U8)
+        nc.vector.tensor_copy(
+            wt_sc[:].bitcast(I32).rearrange("p (a t g m) -> p a t g m", a=PASSES, t=PACK, g=GROUPS),
+            wt_sc_raw[:].bitcast(I32).rearrange("p (a g t m) -> p a t g m", a=PASSES, t=PACK, g=GROUPS),
+        )
         for a in range(PASSES):
             nc.vector.tensor_copy(
                 wt_codes[:, a, :].rearrange("p (t g m) -> p t g m", t=PACK, m=RUN),
                 wt_raw[:, a, :].rearrange("p (g t m) -> p t g m", t=PACK, m=RUN),
             )
-        nc.vector.tensor_copy(
-            wt_sc[:].bitcast(I32).rearrange("p (a t g m) -> p a t g m", a=PASSES, t=PACK, g=GROUPS),
-            wt_sc_raw[:].bitcast(I32).rearrange("p (a g t m) -> p a t g m", a=PASSES, t=PACK, g=GROUPS),
-        )
-
         ws_q.append(quantise("ws1", ws_bf[1], R))
-        parted.append(part_words(1, pick_words(1, "ws_bf1"), None))
+        picked = [at("picked_w1%d" % side, [P, HALF], U32, side * HALF * 4) for side in range(2)]
+        pick_words(1, picked)
+        parted.append(part_words(1, picked))
 
-        wgo_sb = sb("wgo_sb", [P, J], F32, tag="ws_raw0")
+        gates = [sb("gates%d" % n, [P, T], F32, tag=tag) for n, tag in enumerate(("ws_raw0", "wt_raw", "wt_sc_raw", "tab_w"))]
+        wgo_sb = sb("wgo_sb", [P, J], F32, tag="picked_w00")
+        nc.sync.dma_start(gates[0][:], gT[0:P, :])
         nc.sync.dma_start(wgo_sb[:], wgo)
-        gates = []
-        for n, tag in enumerate(("wt_raw", "wt_sc_raw", "ws_raw1", "tab_w")):
-            gates.append(sb("gates%d" % n, [P, T], F32, tag=tag))
+        for n in range(1, PAGES):
             nc.sync.dma_start(gates[n][:], gT[n * P : (n + 1) * P, :])
 
         wd_bf = sb("wd_bf", [P, N * PACK], BF16)
         nc.scalar.copy(wd_bf[:].rearrange("p (n t) -> p n t", t=PACK), wd_raw[:].rearrange("p t n -> p n t"))
         wd_codes, wd_sc = quantise("wd", wd_bf, N)
 
-        def clear_page(tag):
-            page = sb("page%d" % len(pages), [P, T], F32, tag=tag)
-            for c in range(2):
-                nc.gpsimd.memset(page[:, c * J : (c + 1) * J], 0.0)
-            pages.append(page)
-
-        clear_page("ws_bf1")
-        clear_page("wd_bf")
-
         def first_product(h):
             banks = [psum.tile([P, HALF], F32, name="a%d%d" % (h, t), tag="bank%d" % (PACK * h + t)) for t in range(PACK)]
-            order = [(1, 0), (1, 1), (0, 0), (0, 1)]
-            for t in range(PACK):
-                cols = slice(t * P, (t + 1) * P)
-                for step, (side, a) in enumerate(order):
+            order = [(0, 0), (1, 0), (1, 1), (0, 1)]
+            for step, (side, a) in enumerate(order):
+                for t in range(PACK):
+                    cols = slice(t * P, (t + 1) * P)
                     if side == 0:
                         w_codes, w_sc = ws_q[a][0][:, cols], ws_q[a][1][:, cols]
                     else:
@@ -174,7 +170,7 @@ def tile_list_msg_gelu_gate_kernel(
                         out=banks[t][:],
                         lhsT=w_codes.bitcast(FP8X4),
                         lhsT_scale=w_sc,
-                        rhs=parted[h][:, (2 * side + a) * 2 * HALF : (2 * side + a + 1) * 2 * HALF].bitcast(FP4X4),
+                        rhs=parted[h][side][:, a * 2 * HALF : (a + 1) * 2 * HALF].bitcast(FP4X4),
                         rhs_scale=tab_planes[:, (2 * a + side) * J + h * HALF : (2 * a + side) * J + (h + 1) * HALF],
                         start=(step == 0),
                         stop=(step == len(order) - 1),
@@ -182,7 +178,7 @@ def tile_list_msg_gelu_gate_kernel(
             return banks
 
         def hidden(h, banks):
-            act = sb("act%d" % h, [P, PACK, HALF], F32)
+            act = sb("act%d" % h, [P, PACK, HALF], F32, tag="act")
             rounded = sb("rounded%d" % h, [P, PACK, HALF], BF16)
             for t in range(PACK):
                 nc.scalar.activation(act[:, t, :], banks[t][:], ACT.Gelu_apprx_tanh)
@@ -192,54 +188,47 @@ def tile_list_msg_gelu_gate_kernel(
             nc.scalar.copy(grouped[:].rearrange("p (j t) -> p j t", t=PACK), rounded[:].rearrange("p t j -> p j t"))
             return grouped
 
-        def second_product(h, h_codes, h_sc):
-            msgs = []
-            for n in range(PAGES):
-                bank = psum.tile([P, HALF], F32, name="y%d%d" % (h, n), tag="bank%d" % (PACK * h + n))
-                nc.tensor.matmul_mx(
-                    out=bank[:],
-                    lhsT=wd_codes[:, n * P : (n + 1) * P].bitcast(FP8X4),
-                    lhsT_scale=wd_sc[:, n * P : (n + 1) * P],
-                    rhs=h_codes[:].bitcast(FP8X4),
-                    rhs_scale=h_sc[:],
-                    start=True,
-                    stop=True,
-                )
-                msg = sb("msg%d%d" % (h, n), [P, HALF], F32)
-                nc.scalar.copy(msg[:], bank[:])
-                msgs.append(msg)
-            return msgs
+        def message(h, n, h_codes, h_sc, tag=None):
+            bank = psum.tile([P, HALF], F32, name="y%d%d" % (h, n), tag="bank%d" % (PACK * h + n))
+            nc.tensor.matmul_mx(
+                out=bank[:],
+                lhsT=wd_codes[:, n * P : (n + 1) * P].bitcast(FP8X4),
+                lhsT_scale=wd_sc[:, n * P : (n + 1) * P],
+                rhs=h_codes[:].bitcast(FP8X4),
+                rhs_scale=h_sc[:],
+                start=True,
+                stop=True,
+            )
+            msg = sb("msg%d%d" % (h, n), [P, HALF], F32, tag=tag)
+            return bank, msg
 
         sums = [first_product(h) for h in range(HALVES)]
 
-        weighted = {}
-
-        def weigh_gates(name, parts, tag):
-            held = sb(name, [P, len(parts) * HALF], F32, tag=tag)
-            for c, (h, n) in enumerate(parts):
-                weighted[h, n] = held[:, c * HALF : (c + 1) * HALF]
-                nc.vector.tensor_tensor(
-                    weighted[h, n],
-                    gates[n][:].indirect(lists[0][:, h * COLS : (h + 1) * COLS]),
-                    wgo_sb[:, h * HALF : (h + 1) * HALF],
-                    MULT,
-                )
+        def weigh_gates(n, tag=None):
+            held = sb("gate_w%d" % n, [P, J], F32, tag=tag)
+            nc.vector.tensor_tensor(held[:], gates[n][:].indirect(lists[0][:]), wgo_sb[:], MULT)
+            return held
 
         def place(h, n, msg):
-            nc.vector.tensor_tensor(pages[n][:].indirect(lists[1][:, h * COLS : (h + 1) * COLS]), msg[:], weighted[h, n], MULT)
+            nc.vector.tensor_tensor(
+                pages[n][:].indirect(lists[1][:, h * COLS : (h + 1) * COLS]), msg[:], weighted[n][:, h * HALF : (h + 1) * HALF], MULT
+            )
 
-        weigh_gates("gate_w_early", [(0, 0), (1, 0), (0, 1), (1, 1), (0, 2)], None)
+        last = PAGES - 1
+        weighted = [weigh_gates(n) for n in range(last)]
         h_codes, h_sc = quantise("h0", hidden(0, sums[0]), HALF)
-        weigh_gates("gate_w_mid", [(1, 2), (1, 3)], "h_bf0")
-        clear_page("ws_raw1")
-        msgs = [second_product(0, h_codes, h_sc)]
-        for n in range(PAGES - 1):
-            place(0, n, msgs[0][n])
-        h_codes, h_sc = quantise("h1", hidden(1, sums[1]), HALF)
-        weigh_gates("gate_w_late", [(0, 3)], "h_bf1")
-        msgs.append(second_product(1, h_codes, h_sc))
-        place(0, PAGES - 1, msgs[0][PAGES - 1])
+        weighted.append(weigh_gates(last, "rounded0"))
+        made = [message(0, n, h_codes, h_sc) for n in range(last)]
+        for n, (bank, msg) in enumerate(made):
+            nc.scalar.copy(msg[:], bank[:])
+            place(0, n, msg)
+        grouped = hidden(1, sums[1])
+        bank, msg = message(0, last, h_codes, h_sc, "rounded1")
+        h_codes, h_sc = quantise("h1", grouped, HALF)
+        nc.scalar.copy(msg[:], bank[:])
+        place(0, last, msg)
         for n in range(PAGES):
-            place(1, n, msgs[1][n])
-        for n in range(PAGES):
+            bank, msg = message(1, n, h_codes, h_sc)
+            nc.scalar.copy(msg[:], bank[:])
+            place(1, n, msg)
             nc.sync.dma_start(out[n * P : (n + 1) * P, :], pages[n][:])

@@ -24,6 +24,7 @@ HALF = 512
 HALVES = J // HALF
 COLS = HALF // 16
 RUN = 8
+LINE = 4
 GROUPS = R // (PACK * RUN)
 PAGES = N // P
 
@@ -47,26 +48,16 @@ def tile_list_msg_gelu_gate_kernel(
         tab_sc = sb("tab_sc", [P, T], U8)
         wt_sc_raw = sb("wt_sc_raw", [P, PASSES * R], U8)
         tab_planes = sb("tab_planes", [P, PASSES * 2 * J], U8)
-        pages = [sb("page%d" % n, [P, T], F32) for n in range(PAGES)]
+        windows = [sb("window0", [P, T], F32)]
 
+        nc.vector.memset(wt_sc_raw[:].bitcast(I32), 0)
         nc.vector.memset(tab_sc[0:96, :].bitcast(I32), 0)
         nc.vector.memset(tab_planes[:].bitcast(I32), 0)
-        nc.vector.memset(pages[0][:], 0.0)
+        nc.vector.memset(windows[0][:].bitcast(I32), 0)
 
-        nc.gpsimd.memset(wt_sc_raw[:].bitcast(I32), 0)
-        for q in range(QUADS):
-            nc.gpsimd.dma_start(
-                wt_sc_raw[32 * q : 32 * q + 4, :].bitcast(I32).rearrange("p (a r) -> p a r", a=PASSES),
-                wt_scales[:, 4 * q : 4 * q + 4, :].bitcast(I32).rearrange("a p r -> p a r"),
-            )
-        for n in range(1, PAGES):
-            for c in range(2):
-                nc.gpsimd.memset(pages[n][:, c * J : (c + 1) * J], 0.0)
-        sm_sb = [sb("sm_sb%d" % t, [P, 1], F32) for t in range(PACK)]
-        sm_rows = sm.rearrange("(g t m) -> t g m", t=PACK, m=RUN)
-        with nc.allow_non_contiguous_dma(reason="one smoothing factor a partition"):
-            for t in range(PACK):
-                nc.gpsimd.dma_start(sm_sb[t][:], sm_rows[t].unsqueeze(2))
+        warm = sb("warm", [P, 2], F32)
+        nc.gpsimd.memset(warm[:, 0:1], 0.0)
+        nc.scalar.activation(warm[:, 1:2], warm[:, 0:1], ACT.Gelu_apprx_tanh)
 
         nc.sync.dma_start(lists[0][:], offs)
         nc.sync.dma_start(tab_sc[96:P, :].bitcast(I32), tab_scales.rearrange("a q t -> q a t").bitcast(I32))
@@ -77,6 +68,11 @@ def tile_list_msg_gelu_gate_kernel(
         nc.sync.dma_start(ws_raw[0][:], ws_rows[0])
         tab_w = sb("tab_w", [P, T], I32)
         nc.sync.dma_start(tab_w[:], tab_words[0].rearrange("p t b -> p (t b)").bitcast(I32))
+        for q in range(QUADS):
+            nc.sync.dma_start(
+                wt_sc_raw[32 * q : 32 * q + 4, :].bitcast(I32).rearrange("p (a r) -> p a r", a=PASSES),
+                wt_scales[:, 4 * q : 4 * q + 4, :].bitcast(I32).rearrange("a p r -> p a r"),
+            )
         nc.sync.dma_start(ws_raw[1][:], ws_rows[1])
         wt_raw = sb("wt_raw", [P, PASSES, R], I32)
         nc.sync.dma_start(wt_raw[:], wt_words.rearrange("a p r b -> p a (r b)").bitcast(I32))
@@ -97,10 +93,11 @@ def tile_list_msg_gelu_gate_kernel(
 
         def round_ws(a):
             grouped = sb("ws_bf%d" % a, [P, R * PACK], BF16)
-            nc.scalar.copy(
-                grouped[:].rearrange("p (t g m i) -> p t g m i", t=PACK, g=GROUPS, m=RUN),
-                ws_raw[a][:].rearrange("p i (g t m) -> p t g m i", t=PACK, m=RUN),
-            )
+            for u in range(RUN // LINE):
+                nc.scalar.copy(
+                    grouped[:].rearrange("p (t g u c i) -> p u t g i c", t=PACK, g=GROUPS, c=LINE, i=PACK)[:, u],
+                    ws_raw[a][:].rearrange("p i (g t u c) -> p u t g i c", t=PACK, g=GROUPS, c=LINE)[:, u],
+                )
             return grouped
 
         def quantise(name, grouped, width):
@@ -134,12 +131,13 @@ def tile_list_msg_gelu_gate_kernel(
             wt_sc[:].bitcast(I32).rearrange("p (a t g m) -> p a t g m", a=PASSES, t=PACK, g=GROUPS),
             wt_sc_raw[:].bitcast(I32).rearrange("p (a g t m) -> p a t g m", a=PASSES, t=PACK, g=GROUPS),
         )
-        for a in range(PASSES):
-            nc.vector.tensor_copy(
-                wt_codes[:, a, :].rearrange("p (t g m) -> p t g m", t=PACK, m=RUN),
-                wt_raw[:, a, :].rearrange("p (g t m) -> p t g m", t=PACK, m=RUN),
-            )
+        nc.vector.tensor_copy(
+            wt_codes[:].rearrange("p a (t g m) -> p a t g m", t=PACK, m=RUN),
+            wt_raw[:].rearrange("p a (g t m) -> p a t g m", t=PACK, m=RUN),
+        )
         ws_q.append(quantise("ws1", ws_bf[1], R))
+        windows.append(at("window1", [P, T], F32, 6144))
+        nc.vector.memset(windows[1][:].bitcast(I32), 0)
         picked = [at("picked_w1%d" % side, [P, HALF], U32, side * HALF * 4) for side in range(2)]
         pick_words(1, picked)
         parted.append(part_words(1, picked))
@@ -148,12 +146,19 @@ def tile_list_msg_gelu_gate_kernel(
         wgo_sb = sb("wgo_sb", [P, J], F32, tag="picked_w00")
         nc.sync.dma_start(gates[0][:], gT[0:P, :])
         nc.sync.dma_start(wgo_sb[:], wgo)
+        sm_sb = [at("sm_sb%d" % t, [P, 1], F32, 4096 + 64 * t) for t in range(PACK)]
+        sm_rows = sm.rearrange("(g t m) -> t g m", t=PACK, m=RUN)
+        with nc.allow_non_contiguous_dma(reason="one smoothing factor a partition"):
+            for t in range(PACK):
+                nc.sync.dma_start(sm_sb[t][:], sm_rows[t].unsqueeze(2))
         for n in range(1, PAGES):
             nc.sync.dma_start(gates[n][:], gT[n * P : (n + 1) * P, :])
 
         wd_bf = sb("wd_bf", [P, N * PACK], BF16)
-        nc.scalar.copy(wd_bf[:].rearrange("p (n t) -> p n t", t=PACK), wd_raw[:].rearrange("p t n -> p n t"))
+        nc.scalar.copy(wd_bf[:].rearrange("p (n c t) -> p n t c", t=PACK, c=LINE), wd_raw[:].rearrange("p t (n c) -> p n t c", c=LINE))
         wd_codes, wd_sc = quantise("wd", wd_bf, N)
+        windows.append(sb("window2", [P, T], F32, tag="tab_sc"))
+        nc.vector.memset(windows[2][:].bitcast(I32), 0)
 
         def first_product(h):
             banks = [psum.tile([P, HALF], F32, name="a%d%d" % (h, t), tag="bank%d" % (PACK * h + t)) for t in range(PACK)]
@@ -185,10 +190,10 @@ def tile_list_msg_gelu_gate_kernel(
             for t in range(PACK):
                 nc.scalar.activation(rounded[:, t, :], act[:, t, :], ACT.Copy, scale=sm_sb[t][:])
             grouped = sb("h_bf%d" % h, [P, HALF * PACK], BF16)
-            nc.scalar.copy(grouped[:].rearrange("p (j t) -> p j t", t=PACK), rounded[:].rearrange("p t j -> p j t"))
+            nc.scalar.copy(grouped[:].rearrange("p (j c t) -> p j t c", t=PACK, c=LINE), rounded[:].rearrange("p t (j c) -> p j t c", c=LINE))
             return grouped
 
-        def message(h, n, h_codes, h_sc, tag=None):
+        def message(h, n, h_codes, h_sc, msg):
             bank = psum.tile([P, HALF], F32, name="y%d%d" % (h, n), tag="bank%d" % (PACK * h + n))
             nc.tensor.matmul_mx(
                 out=bank[:],
@@ -199,8 +204,7 @@ def tile_list_msg_gelu_gate_kernel(
                 start=True,
                 stop=True,
             )
-            msg = sb("msg%d%d" % (h, n), [P, HALF], F32, tag=tag)
-            return bank, msg
+            nc.scalar.copy(msg, bank[:])
 
         sums = [first_product(h) for h in range(HALVES)]
 
@@ -209,26 +213,26 @@ def tile_list_msg_gelu_gate_kernel(
             nc.vector.tensor_tensor(held[:], gates[n][:].indirect(lists[0][:]), wgo_sb[:], MULT)
             return held
 
-        def place(h, n, msg):
+        def place(h, n, h_codes, h_sc, tag=None):
+            msg = sb("msg%d%d" % (h, n), [P, HALF], F32, tag=tag)
+            message(h, n, h_codes, h_sc, msg[:])
             nc.vector.tensor_tensor(
-                pages[n][:].indirect(lists[1][:, h * COLS : (h + 1) * COLS]), msg[:], weighted[n][:, h * HALF : (h + 1) * HALF], MULT
+                windows[n][:].indirect(lists[1][:, h * COLS : (h + 1) * COLS]), msg[:], weighted[n][:, h * HALF : (h + 1) * HALF], MULT
             )
 
         last = PAGES - 1
         weighted = [weigh_gates(n) for n in range(last)]
-        h_codes, h_sc = quantise("h0", hidden(0, sums[0]), HALF)
+        h_q = [quantise("h0", hidden(0, sums[0]), HALF)]
         weighted.append(weigh_gates(last, "rounded0"))
-        made = [message(0, n, h_codes, h_sc) for n in range(last)]
-        for n, (bank, msg) in enumerate(made):
-            nc.scalar.copy(msg[:], bank[:])
-            place(0, n, msg)
-        grouped = hidden(1, sums[1])
-        bank, msg = message(0, last, h_codes, h_sc, "rounded1")
-        h_codes, h_sc = quantise("h1", grouped, HALF)
-        nc.scalar.copy(msg[:], bank[:])
-        place(0, last, msg)
-        for n in range(PAGES):
-            bank, msg = message(1, n, h_codes, h_sc)
-            nc.scalar.copy(msg[:], bank[:])
-            place(1, n, msg)
-            nc.sync.dma_start(out[n * P : (n + 1) * P, :], pages[n][:])
+        for n in range(last - 1):
+            place(0, n, *h_q[0])
+        h_q.append(quantise("h1", hidden(1, sums[1]), HALF))
+        place(0, last - 1, *h_q[0], tag="rounded1")
+        for n in range(last):
+            place(1, n, *h_q[1])
+            nc.sync.dma_start(out[n * P : (n + 1) * P, :], windows[n][:])
+        msg = sb("msg_last", [P, J], F32)
+        for h in range(HALVES):
+            message(h, last, *h_q[h], msg[:, h * HALF : (h + 1) * HALF])
+        nc.vector.tensor_tensor(windows[0][:].indirect(lists[1][:]), msg[:], weighted[last][:], MULT)
+        nc.sync.dma_start(out[last * P : (last + 1) * P, :], windows[0][:])

@@ -45,25 +45,27 @@ def tile_list_msg_gelu_gate_kernel(
             return laid.tile(shape, dtype, name=name, tag=name, align_bytes=64, offset=offset)
 
         lists = [keep.tile([P, J // 16], U16, name="src_list"), keep.tile([P, J // 16], U16, name="dst_list")]
-        tab_sc = sb("tab_sc", [P, T], U8)
+        tab_sc = at("tab_sc", [P, T], U8, 15360)
         wt_sc_raw = sb("wt_sc_raw", [P, PASSES * R], U8)
         tab_planes = sb("tab_planes", [P, PASSES * 2 * J], U8)
-        windows = [sb("window0", [P, T], F32)]
-
-        nc.vector.memset(wt_sc_raw[:].bitcast(I32), 0)
-        nc.vector.memset(tab_sc[0:96, :].bitcast(I32), 0)
-        nc.vector.memset(tab_planes[:].bitcast(I32), 0)
-        nc.vector.memset(windows[0][:].bitcast(I32), 0)
+        windows = [sb("window%d" % n, [P, T], F32) for n in range(PAGES - 1)]
 
         warm = sb("warm", [P, 2], F32)
         nc.gpsimd.memset(warm[:, 0:1], 0.0)
         nc.scalar.activation(warm[:, 1:2], warm[:, 0:1], ACT.Gelu_apprx_tanh)
 
+        nc.gpsimd.memset(wt_sc_raw[:].bitcast(I32), 0)
+        nc.gpsimd.memset(tab_sc[0:96, :].bitcast(I32), 0)
+        nc.vector.memset(windows[0][:].bitcast(I32), 0)
+        nc.gpsimd.memset(tab_planes[:].bitcast(I32), 0)
+        for window in windows[1:]:
+            nc.gpsimd.memset(window[:].bitcast(I32), 0)
+
         nc.sync.dma_start(lists[0][:], offs)
         nc.sync.dma_start(tab_sc[96:P, :].bitcast(I32), tab_scales.rearrange("a q t -> q a t").bitcast(I32))
         nc.sync.dma_start(lists[1][:], offs2)
 
-        ws_raw = [sb("ws_raw0", [P, PACK, R], F32), at("ws_raw1", [P, PACK, R], F32, 0)]
+        ws_raw = [at("ws_raw0", [P, PACK, R], F32, 26624), at("ws_raw1", [P, PACK, R], F32, 0)]
         ws_rows = ws.rearrange("(a p i) r -> a p i r", a=PASSES, i=PACK)
         nc.sync.dma_start(ws_raw[0][:], ws_rows[0])
         tab_w = sb("tab_w", [P, T], I32)
@@ -86,13 +88,13 @@ def tile_list_msg_gelu_gate_kernel(
                 picked_sc[96 + 8 * q : 96 + 8 * q + 8, :].bitcast(I32),
             )
 
-        wd_raw = sb("wd_raw", [P, PACK, N], F32, tag="tab_sc")
+        wd_raw = at("wd_raw", [P, PACK, N], F32, 8192)
         wd_rows = wd.rearrange("(g t i) n -> t g i n", t=PACK, i=RUN)
         for t in range(PACK):
             nc.sync.dma_start(wd_raw[:, t, :], wd_rows[t])
 
         def round_ws(a):
-            grouped = sb("ws_bf%d" % a, [P, R * PACK], BF16)
+            grouped = at("ws_bf%d" % a, [P, R * PACK], BF16, (43008, 53248)[a])
             for u in range(RUN // LINE):
                 nc.scalar.copy(
                     grouped[:].rearrange("p (t g u c i) -> p u t g i c", t=PACK, g=GROUPS, c=LINE, i=PACK)[:, u],
@@ -100,8 +102,8 @@ def tile_list_msg_gelu_gate_kernel(
                 )
             return grouped
 
-        def quantise(name, grouped, width):
-            codes = sb(name + "_codes", [P, width], U32)
+        def quantise(name, grouped, width, offset=None):
+            codes = sb(name + "_codes", [P, width], U32) if offset is None else at(name + "_codes", [P, width], U32, offset)
             scales = sb(name + "_sc", [P, width], U8)
             nc.vector.quantize_mx(out=codes[:].bitcast(FP8X4), scales=scales[:], in_=grouped[:])
             return codes, scales
@@ -136,35 +138,33 @@ def tile_list_msg_gelu_gate_kernel(
             wt_raw[:].rearrange("p a (g t m) -> p a t g m", t=PACK, m=RUN),
         )
         ws_q.append(quantise("ws1", ws_bf[1], R))
-        windows.append(at("window1", [P, T], F32, 6144))
-        nc.vector.memset(windows[1][:].bitcast(I32), 0)
         picked = [at("picked_w1%d" % side, [P, HALF], U32, side * HALF * 4) for side in range(2)]
         pick_words(1, picked)
         parted.append(part_words(1, picked))
 
-        gates = [sb("gates%d" % n, [P, T], F32, tag=tag) for n, tag in enumerate(("ws_raw0", "wt_raw", "wt_sc_raw", "tab_w"))]
-        wgo_sb = sb("wgo_sb", [P, J], F32, tag="picked_w00")
-        nc.sync.dma_start(gates[0][:], gT[0:P, :])
+        gates = [at("gates%d" % n, [P, T], F32, offset) for n, offset in enumerate((45056, 16384, 28672, 36864))]
+        wgo_sb = at("wgo_sb", [P, J], F32, 24576)
+        nc.sync.dma_start(gates[1][:], gT[P : 2 * P, :])
         nc.sync.dma_start(wgo_sb[:], wgo)
         sm_sb = [at("sm_sb%d" % t, [P, 1], F32, 4096 + 64 * t) for t in range(PACK)]
         sm_rows = sm.rearrange("(g t m) -> t g m", t=PACK, m=RUN)
         with nc.allow_non_contiguous_dma(reason="one smoothing factor a partition"):
             for t in range(PACK):
                 nc.sync.dma_start(sm_sb[t][:], sm_rows[t].unsqueeze(2))
-        for n in range(1, PAGES):
+        for n in (2, 3, 0):
             nc.sync.dma_start(gates[n][:], gT[n * P : (n + 1) * P, :])
 
         wd_bf = sb("wd_bf", [P, N * PACK], BF16)
         nc.scalar.copy(wd_bf[:].rearrange("p (n c t) -> p n t c", t=PACK, c=LINE), wd_raw[:].rearrange("p t (n c) -> p n t c", c=LINE))
         wd_codes, wd_sc = quantise("wd", wd_bf, N)
-        windows.append(sb("window2", [P, T], F32, tag="tab_sc"))
-        nc.vector.memset(windows[2][:].bitcast(I32), 0)
 
         def first_product(h):
             banks = [psum.tile([P, HALF], F32, name="a%d%d" % (h, t), tag="bank%d" % (PACK * h + t)) for t in range(PACK)]
             order = [(0, 0), (1, 0), (1, 1), (0, 1)]
-            for step, (side, a) in enumerate(order):
-                for t in range(PACK):
+            steps = [(0, t) for t in range(PACK)] + [(step, t) for t in range(PACK) for step in range(1, len(order))]
+            for step, t in steps:
+                if True:
+                    side, a = order[step]
                     cols = slice(t * P, (t + 1) * P)
                     if side == 0:
                         w_codes, w_sc = ws_q[a][0][:, cols], ws_q[a][1][:, cols]
@@ -183,8 +183,8 @@ def tile_list_msg_gelu_gate_kernel(
             return banks
 
         def hidden(h, banks):
-            act = sb("act%d" % h, [P, PACK, HALF], F32, tag="act")
-            rounded = sb("rounded%d" % h, [P, PACK, HALF], BF16)
+            act = at("act%d" % h, [P, PACK, HALF], F32, 8192)
+            rounded = sb("rounded%d" % h, [P, PACK, HALF], BF16, tag=("rounded0", "h_bf0")[h])
             for t in range(PACK):
                 nc.scalar.activation(act[:, t, :], banks[t][:], ACT.Gelu_apprx_tanh)
             for t in range(PACK):
@@ -221,13 +221,20 @@ def tile_list_msg_gelu_gate_kernel(
             )
 
         last = PAGES - 1
-        weighted = [weigh_gates(n) for n in range(last)]
-        h_q = [quantise("h0", hidden(0, sums[0]), HALF)]
-        weighted.append(weigh_gates(last, "rounded0"))
+        weighted = [None] + [weigh_gates(n) for n in range(1, PAGES)]
+        h_q = [quantise("h0", hidden(0, sums[0]), HALF, 36864)]
+        weighted[0] = sb("gate_w0", [P, J], F32, tag="rounded0")
+        for h in range(HALVES):
+            nc.vector.tensor_tensor(
+                weighted[0][:, h * HALF : (h + 1) * HALF],
+                gates[0][:].indirect(lists[0][:, h * COLS : (h + 1) * COLS]),
+                wgo_sb[:, h * HALF : (h + 1) * HALF],
+                MULT,
+            )
         for n in range(last - 1):
             place(0, n, *h_q[0])
         h_q.append(quantise("h1", hidden(1, sums[1]), HALF))
-        place(0, last - 1, *h_q[0], tag="rounded1")
+        place(0, last - 1, *h_q[0], tag="h_bf0")
         for n in range(last):
             place(1, n, *h_q[1])
             nc.sync.dma_start(out[n * P : (n + 1) * P, :], windows[n][:])

@@ -48,18 +48,16 @@ def tile_list_msg_gelu_gate_kernel(
         tab_sc = at("tab_sc", [P, T], U8, 15360)
         wt_sc_raw = sb("wt_sc_raw", [P, PASSES * R], U8)
         tab_planes = sb("tab_planes", [P, PASSES * 2 * J], U8)
-        windows = [sb("window%d" % n, [P, T], F32) for n in range(PAGES - 1)]
+        windows = [sb("window0", [P, T], F32)]
 
         warm = sb("warm", [P, 2], F32)
         nc.gpsimd.memset(warm[:, 0:1], 0.0)
         nc.scalar.activation(warm[:, 1:2], warm[:, 0:1], ACT.Gelu_apprx_tanh)
 
-        nc.gpsimd.memset(wt_sc_raw[:].bitcast(I32), 0)
-        nc.gpsimd.memset(tab_sc[0:96, :].bitcast(I32), 0)
+        nc.vector.memset(wt_sc_raw[:].bitcast(I32), 0)
+        nc.vector.memset(tab_sc[0:96, :].bitcast(I32), 0)
+        nc.vector.memset(tab_planes[:].bitcast(I32), 0)
         nc.vector.memset(windows[0][:].bitcast(I32), 0)
-        nc.gpsimd.memset(tab_planes[:].bitcast(I32), 0)
-        for window in windows[1:]:
-            nc.gpsimd.memset(window[:].bitcast(I32), 0)
 
         nc.sync.dma_start(lists[0][:], offs)
         nc.sync.dma_start(tab_sc[96:P, :].bitcast(I32), tab_scales.rearrange("a q t -> q a t").bitcast(I32))
@@ -231,6 +229,9 @@ def tile_list_msg_gelu_gate_kernel(
                 wgo_sb[:, h * HALF : (h + 1) * HALF],
                 MULT,
             )
+        for n, offset in ((1, 16384), (2, 45056)):
+            windows.append(at("window%d" % n, [P, T], F32, offset))
+            nc.gpsimd.memset(windows[n][:].bitcast(I32), 0)
         for n in range(last - 1):
             place(0, n, *h_q[0])
         h_q.append(quantise("h1", hidden(1, sums[1]), HALF))

@@ -23,9 +23,7 @@ QUADS = 4
 HALF = 512
 HALVES = J // HALF
 COLS = HALF // 16
-RUN = 8
 LINE = 4
-GROUPS = R // (PACK * RUN)
 PAGES = N // P
 
 
@@ -65,9 +63,9 @@ def tile_list_msg_gelu_gate_kernel(
 
         ws_raw = [at("ws_raw0", [P, PACK, R], F32, 26624), at("ws_raw1", [P, PACK, R], F32, 0)]
         ws_rows = ws.rearrange("(a p i) r -> a p i r", a=PASSES, i=PACK)
-        nc.sync.dma_start(ws_raw[0][:], ws_rows[0])
         tab_w = sb("tab_w", [P, T], I32)
         nc.sync.dma_start(tab_w[:], tab_words[0].rearrange("p t b -> p (t b)").bitcast(I32))
+        nc.sync.dma_start(ws_raw[0][:], ws_rows[0])
         for q in range(QUADS):
             nc.sync.dma_start(
                 wt_sc_raw[32 * q : 32 * q + 4, :].bitcast(I32).rearrange("p (a r) -> p a r", a=PASSES),
@@ -87,17 +85,14 @@ def tile_list_msg_gelu_gate_kernel(
             )
 
         wd_raw = at("wd_raw", [P, PACK, N], F32, 8192)
-        wd_rows = wd.rearrange("(g t i) n -> t g i n", t=PACK, i=RUN)
-        for t in range(PACK):
-            nc.sync.dma_start(wd_raw[:, t, :], wd_rows[t])
+        nc.sync.dma_start(wd_raw[:], wd.rearrange("(p t) n -> p t n", t=PACK))
 
         def round_ws(a):
-            grouped = at("ws_bf%d" % a, [P, R * PACK], BF16, (43008, 53248)[a])
-            for u in range(RUN // LINE):
-                nc.scalar.copy(
-                    grouped[:].rearrange("p (t g u c i) -> p u t g i c", t=PACK, g=GROUPS, c=LINE, i=PACK)[:, u],
-                    ws_raw[a][:].rearrange("p i (g t u c) -> p u t g i c", t=PACK, g=GROUPS, c=LINE)[:, u],
-                )
+            grouped = at("ws_bf%d" % a, [P, R * PACK], BF16, (43008, 53312)[a])
+            nc.scalar.copy(
+                grouped[:].rearrange("p (t m i) -> p m i t", t=PACK, i=PACK),
+                ws_raw[a][:].rearrange("p i (m t) -> p m i t", t=PACK),
+            )
             return grouped
 
         def quantise(name, grouped, width, offset=None):
@@ -128,27 +123,24 @@ def tile_list_msg_gelu_gate_kernel(
         wt_codes = sb("wt_codes", [P, PASSES, R], I32)
         wt_sc = sb("wt_sc", [P, PASSES * R], U8)
         nc.vector.tensor_copy(
-            wt_sc[:].bitcast(I32).rearrange("p (a t g m) -> p a t g m", a=PASSES, t=PACK, g=GROUPS),
-            wt_sc_raw[:].bitcast(I32).rearrange("p (a g t m) -> p a t g m", a=PASSES, t=PACK, g=GROUPS),
+            wt_sc[:].rearrange("p (a t m) -> p a t m", a=PASSES, t=PACK),
+            wt_sc_raw[:].rearrange("p (a m t) -> p a t m", a=PASSES, t=PACK),
         )
         nc.vector.tensor_copy(
-            wt_codes[:].rearrange("p a (t g m) -> p a t g m", t=PACK, m=RUN),
-            wt_raw[:].rearrange("p a (g t m) -> p a t g m", t=PACK, m=RUN),
+            wt_codes[:].rearrange("p a (t m) -> p a m t", t=PACK),
+            wt_raw[:].rearrange("p a (m t) -> p a m t", t=PACK),
         )
         ws_q.append(quantise("ws1", ws_bf[1], R))
         picked = [at("picked_w1%d" % side, [P, HALF], U32, side * HALF * 4) for side in range(2)]
         pick_words(1, picked)
         parted.append(part_words(1, picked))
 
-        gates = [at("gates%d" % n, [P, T], F32, offset) for n, offset in enumerate((45056, 16384, 28672, 36864))]
+        gates = [at("gates%d" % n, [P, T], F32, offset) for n, offset in enumerate((45120, 16384, 28736, 36928))]
         wgo_sb = at("wgo_sb", [P, J], F32, 24576)
         nc.sync.dma_start(gates[1][:], gT[P : 2 * P, :])
         nc.sync.dma_start(wgo_sb[:], wgo)
-        sm_sb = [at("sm_sb%d" % t, [P, 1], F32, 4096 + 64 * t) for t in range(PACK)]
-        sm_rows = sm.rearrange("(g t m) -> t g m", t=PACK, m=RUN)
-        with nc.allow_non_contiguous_dma(reason="one smoothing factor a partition"):
-            for t in range(PACK):
-                nc.sync.dma_start(sm_sb[t][:], sm_rows[t].unsqueeze(2))
+        sm_sb = at("sm_sb", [P, PACK], F32, 28672)
+        nc.sync.dma_start(sm_sb[:], sm.rearrange("(p t) -> p t", t=PACK))
         for n in (2, 3, 0):
             nc.sync.dma_start(gates[n][:], gT[n * P : (n + 1) * P, :])
 
@@ -186,7 +178,7 @@ def tile_list_msg_gelu_gate_kernel(
             for t in range(PACK):
                 nc.scalar.activation(act[:, t, :], banks[t][:], ACT.Gelu_apprx_tanh)
             for t in range(PACK):
-                nc.scalar.activation(rounded[:, t, :], act[:, t, :], ACT.Copy, scale=sm_sb[t][:])
+                nc.scalar.activation(rounded[:, t, :], act[:, t, :], ACT.Copy, scale=sm_sb[:, t : t + 1])
             grouped = sb("h_bf%d" % h, [P, HALF * PACK], BF16)
             nc.scalar.copy(grouped[:].rearrange("p (j c t) -> p j t c", t=PACK, c=LINE), rounded[:].rearrange("p t (j c) -> p j t c", c=LINE))
             return grouped
@@ -220,7 +212,7 @@ def tile_list_msg_gelu_gate_kernel(
 
         last = PAGES - 1
         weighted = [None] + [weigh_gates(n) for n in range(1, PAGES)]
-        h_q = [quantise("h0", hidden(0, sums[0]), HALF, 36864)]
+        h_q = [quantise("h0", hidden(0, sums[0]), HALF, 36928)]
         weighted[0] = sb("gate_w0", [P, J], F32, tag="rounded0")
         for h in range(HALVES):
             nc.vector.tensor_tensor(
@@ -229,7 +221,7 @@ def tile_list_msg_gelu_gate_kernel(
                 wgo_sb[:, h * HALF : (h + 1) * HALF],
                 MULT,
             )
-        for n, offset in ((1, 16384), (2, 45056)):
+        for n, offset in ((1, 16384), (2, 45120)):
             windows.append(at("window%d" % n, [P, T], F32, offset))
             nc.gpsimd.memset(windows[n][:].bitcast(I32), 0)
         for n in range(last - 1):

@@ -23,6 +23,7 @@ QUADS = 4
 HALF = 512
 HALVES = J // HALF
 COLS = HALF // 16
+PART = HALF // 2
 LINE = 4
 PAGES = N // P
 
@@ -52,8 +53,8 @@ def tile_list_msg_gelu_gate_kernel(
         nc.gpsimd.memset(warm[:, 0:1], 0.0)
         nc.scalar.activation(warm[:, 1:2], warm[:, 0:1], ACT.Gelu_apprx_tanh)
 
-        nc.vector.memset(wt_sc_raw[:].bitcast(I32), 0)
-        nc.vector.memset(tab_sc[0:96, :].bitcast(I32), 0)
+        nc.gpsimd.memset(wt_sc_raw[:].bitcast(I32), 0)
+        nc.gpsimd.memset(tab_sc[0:96, :].bitcast(I32), 0)
         nc.vector.memset(tab_planes[:].bitcast(I32), 0)
         nc.vector.memset(windows[0][:].bitcast(I32), 0)
 
@@ -98,7 +99,7 @@ def tile_list_msg_gelu_gate_kernel(
         def quantise(name, grouped, width, offset=None):
             codes = sb(name + "_codes", [P, width], U32) if offset is None else at(name + "_codes", [P, width], U32, offset)
             scales = sb(name + "_sc", [P, width], U8)
-            nc.vector.quantize_mx(out=codes[:].bitcast(FP8X4), scales=scales[:], in_=grouped[:])
+            nc.vector.quantize_mx(out=codes[:].bitcast(FP8X4), scales=scales[:], in_=grouped)
             return codes, scales
 
         def pick_words(h, picked):
@@ -116,7 +117,7 @@ def tile_list_msg_gelu_gate_kernel(
             return parted
 
         ws_bf = [round_ws(a) for a in range(PASSES)]
-        ws_q = [quantise("ws0", ws_bf[0], R)]
+        ws_q = [quantise("ws0", ws_bf[0][:], R)]
         picked = [sb("picked_w0%d" % side, [P, HALF], U32) for side in range(2)]
         pick_words(0, picked)
         parted = [part_words(0, picked)]
@@ -126,11 +127,11 @@ def tile_list_msg_gelu_gate_kernel(
             wt_sc[:].rearrange("p (a t m) -> p a t m", a=PASSES, t=PACK),
             wt_sc_raw[:].rearrange("p (a m t) -> p a t m", a=PASSES, t=PACK),
         )
-        nc.vector.tensor_copy(
-            wt_codes[:].rearrange("p a (t m) -> p a m t", t=PACK),
-            wt_raw[:].rearrange("p a (m t) -> p a m t", t=PACK),
+        nc.scalar.copy(
+            wt_codes[:].bitcast(U32).rearrange("p a (t m) -> p a m t", t=PACK),
+            wt_raw[:].bitcast(U32).rearrange("p a (m t) -> p a m t", t=PACK),
         )
-        ws_q.append(quantise("ws1", ws_bf[1], R))
+        ws_q.append(quantise("ws1", ws_bf[1][:], R))
         picked = [at("picked_w1%d" % side, [P, HALF], U32, side * HALF * 4) for side in range(2)]
         pick_words(1, picked)
         parted.append(part_words(1, picked))
@@ -146,42 +147,50 @@ def tile_list_msg_gelu_gate_kernel(
 
         wd_bf = sb("wd_bf", [P, N * PACK], BF16)
         nc.scalar.copy(wd_bf[:].rearrange("p (n c t) -> p n t c", t=PACK, c=LINE), wd_raw[:].rearrange("p t (n c) -> p n t c", c=LINE))
-        wd_codes, wd_sc = quantise("wd", wd_bf, N)
+        wd_codes, wd_sc = quantise("wd", wd_bf[:], N)
 
         def first_product(h):
-            banks = [psum.tile([P, HALF], F32, name="a%d%d" % (h, t), tag="bank%d" % (PACK * h + t)) for t in range(PACK)]
-            order = [(0, 0), (1, 0), (1, 1), (0, 1)]
-            steps = [(0, t) for t in range(PACK)] + [(step, t) for t in range(PACK) for step in range(1, len(order))]
-            for step, t in steps:
-                if True:
-                    side, a = order[step]
-                    cols = slice(t * P, (t + 1) * P)
-                    if side == 0:
-                        w_codes, w_sc = ws_q[a][0][:, cols], ws_q[a][1][:, cols]
-                    else:
-                        w_codes = wt_codes[:, a, cols]
-                        w_sc = wt_sc[:, a * R + t * P : a * R + (t + 1) * P]
-                    nc.tensor.matmul_mx(
-                        out=banks[t][:],
-                        lhsT=w_codes.bitcast(FP8X4),
-                        lhsT_scale=w_sc,
-                        rhs=parted[h][side][:, a * 2 * HALF : (a + 1) * 2 * HALF].bitcast(FP4X4),
-                        rhs_scale=tab_planes[:, (2 * a + side) * J + h * HALF : (2 * a + side) * J + (h + 1) * HALF],
-                        start=(step == 0),
-                        stop=(step == len(order) - 1),
-                    )
+            banks = [psum.tile([P, 2, PART], F32, name="a%d%d" % (h, b), tag="bank%d" % (PACK * h + b)) for b in range(PACK)]
+            order = [(0, 0), (0, 1), (1, 0), (1, 1)]
+            steps = [(b, e, 0) for b in range(2) for e in range(2)]
+            steps = steps + [(b, e, step) for b in range(PACK) for step in range(len(order)) for e in range(2) if b > 1 or step > 0]
+            for b, e, step in steps:
+                side, a = order[step]
+                t = 2 * (b % 2) + e
+                cols = slice(t * P, (t + 1) * P)
+                if side == 0:
+                    w_codes, w_sc = ws_q[a][0][:, cols], ws_q[a][1][:, cols]
+                else:
+                    w_codes = wt_codes[:, a, cols]
+                    w_sc = wt_sc[:, a * R + t * P : a * R + (t + 1) * P]
+                first = (b // 2) * PART
+                words = a * HALF + first
+                edges = (2 * a + side) * J + h * HALF + first
+                nc.tensor.matmul_mx(
+                    out=banks[b][:, e, :],
+                    lhsT=w_codes.bitcast(FP8X4),
+                    lhsT_scale=w_sc,
+                    rhs=parted[h][side][:, 2 * words : 2 * (words + PART)].bitcast(FP4X4),
+                    rhs_scale=tab_planes[:, edges : edges + PART],
+                    start=(step == 0 and e == 0),
+                    stop=(step == len(order) - 1 and e == 1),
+                )
             return banks
 
         def hidden(h, banks):
-            act = at("act%d" % h, [P, PACK, HALF], F32, 8192)
-            rounded = sb("rounded%d" % h, [P, PACK, HALF], BF16, tag=("rounded0", "h_bf0")[h])
-            for t in range(PACK):
-                nc.scalar.activation(act[:, t, :], banks[t][:], ACT.Gelu_apprx_tanh)
-            for t in range(PACK):
-                nc.scalar.activation(rounded[:, t, :], act[:, t, :], ACT.Copy, scale=sm_sb[:, t : t + 1])
-            grouped = sb("h_bf%d" % h, [P, HALF * PACK], BF16)
-            nc.scalar.copy(grouped[:].rearrange("p (j c t) -> p j t c", t=PACK, c=LINE), rounded[:].rearrange("p t (j c) -> p j t c", c=LINE))
-            return grouped
+            act = at("act%d" % h, [P, 2, PACK, PART], F32, 8192)
+            rounded = sb("rounded%d" % h, [P, 2, PACK, PART], BF16, tag=("rounded0", "h_bf0")[h])
+            grouped = sb("h_bf%d" % h, [P, 2, PART * PACK], BF16)
+            for q in range(2):
+                for pair in range(2):
+                    nc.scalar.activation(act[:, q, 2 * pair : 2 * pair + 2, :], banks[2 * q + pair][:], ACT.Gelu_apprx_tanh)
+                for t in range(PACK):
+                    nc.scalar.activation(rounded[:, q, t, :], act[:, q, t, :], ACT.Copy, scale=sm_sb[:, t : t + 1])
+                nc.scalar.copy(
+                    grouped[:, q, :].rearrange("p (j c t) -> p j t c", t=PACK, c=LINE),
+                    rounded[:, q].rearrange("p t (j c) -> p j t c", c=LINE),
+                )
+            return grouped[:].rearrange("p q w -> p (q w)")
 
         def message(h, n, h_codes, h_sc, msg):
             bank = psum.tile([P, HALF], F32, name="y%d%d" % (h, n), tag="bank%d" % (PACK * h + n))

@@ -49,10 +49,6 @@ def tile_list_msg_gelu_gate_kernel(
         tab_planes = sb("tab_planes", [P, PASSES * 2 * J], U8)
         windows = [sb("window0", [P, T], F32)]
 
-        warm = sb("warm", [P, 2], F32)
-        nc.gpsimd.memset(warm[:, 0:1], 0.0)
-        nc.scalar.activation(warm[:, 1:2], warm[:, 0:1], ACT.Gelu_apprx_tanh)
-
         nc.gpsimd.memset(wt_sc_raw[:].bitcast(I32), 0)
         nc.gpsimd.memset(tab_sc[0:96, :].bitcast(I32), 0)
         nc.vector.memset(tab_planes[:].bitcast(I32), 0)

@@ -1,6 +1,7 @@
 from contextlib import ExitStack
 
 import concourse.mybir as mybir
+from concourse.masks import make_identity
 
 K, R, N, T, J = 1024, 512, 512, 2048, 1024
 FLOPS = 2 * J * R * (2 * K + N)
@@ -23,9 +24,12 @@ QUADS = 4
 HALF = 512
 HALVES = J // HALF
 COLS = HALF // 16
-PART = HALF // 2
+PART = 2 * P
 LINE = 4
 PAGES = N // P
+WIDE = N // 2
+PAGE_BYTES = T * 4
+LAP = 64
 
 
 def tile_list_msg_gelu_gate_kernel(
@@ -43,34 +47,46 @@ def tile_list_msg_gelu_gate_kernel(
         def at(name, shape, dtype, offset):
             return laid.tile(shape, dtype, name=name, tag=name, align_bytes=64, offset=offset)
 
-        lists = [keep.tile([P, J // 16], U16, name="src_list"), keep.tile([P, J // 16], U16, name="dst_list")]
-        tab_sc = at("tab_sc", [P, T], U8, 15360)
-        wt_sc_raw = sb("wt_sc_raw", [P, PASSES * R], U8)
-        tab_planes = sb("tab_planes", [P, PASSES * 2 * J], U8)
-        windows = [sb("window0", [P, T], F32)]
+        words = HALF * 4
+        tab_sc_at = J * 4 - LAP
+        wt_codes_at = tab_sc_at + 2 * LAP
+        ws_raw0_at = wt_codes_at + PASSES * R * 4 + PAGE_BYTES - LAP
+        gates2_at = ws_raw0_at + LAP + 2 * words
+        ws_bf0_at = gates2_at + 2 * PAGE_BYTES - LAP
+        wd_raw0_at = ws_bf0_at + LAP
+        ws_bf1_at = wd_raw0_at + WIDE * PACK * 4 + PAGE_BYTES
+        wd_raw1_at = ws_bf1_at + LAP
+        ws_raw1_at = wd_raw1_at + WIDE * PACK * 4
+        rounded0_at = ws_raw1_at + words + 2 * PAGE_BYTES - LAP
+        wd_bf1_at = rounded0_at + LAP + PAGE_BYTES
 
-        nc.gpsimd.memset(wt_sc_raw[:].bitcast(I32), 0)
+        lists = [keep.tile([P, J // 16], U16, name="src_list"), keep.tile([P, J // 16], U16, name="dst_list")]
+        tab_sc = at("tab_sc", [P, T], U8, tab_sc_at)
+        wt_sc = sb("wt_sc", [P, PASSES * R], U8)
+        tab_planes = sb("tab_planes", [P, PASSES * 2 * J], U8)
+        ident = sb("ident", [P, P], F32)
+
+        nc.gpsimd.memset(wt_sc[:].bitcast(I32), 0)
         nc.gpsimd.memset(tab_sc[0:96, :].bitcast(I32), 0)
+        make_identity(nc, ident[:])
         nc.vector.memset(tab_planes[:].bitcast(I32), 0)
-        nc.vector.memset(windows[0][:].bitcast(I32), 0)
 
         nc.sync.dma_start(lists[0][:], offs)
         nc.sync.dma_start(tab_sc[96:P, :].bitcast(I32), tab_scales.rearrange("a q t -> q a t").bitcast(I32))
         nc.sync.dma_start(lists[1][:], offs2)
 
-        ws_raw = [at("ws_raw0", [P, PACK, R], F32, 26624), at("ws_raw1", [P, PACK, R], F32, 0)]
+        ws_raw = [at("ws_raw0", [P, PACK, R], F32, ws_raw0_at), at("ws_raw1", [P, PACK, R], F32, ws_raw1_at)]
         ws_rows = ws.rearrange("(a p i) r -> a p i r", a=PASSES, i=PACK)
         tab_w = sb("tab_w", [P, T], I32)
-        nc.sync.dma_start(tab_w[:], tab_words[0].rearrange("p t b -> p (t b)").bitcast(I32))
         nc.sync.dma_start(ws_raw[0][:], ws_rows[0])
+        nc.sync.dma_start(tab_w[:], tab_words[0].rearrange("p t b -> p (t b)").bitcast(I32))
         for q in range(QUADS):
             nc.sync.dma_start(
-                wt_sc_raw[32 * q : 32 * q + 4, :].bitcast(I32).rearrange("p (a r) -> p a r", a=PASSES),
+                wt_sc[32 * q : 32 * q + 4, :].bitcast(I32).rearrange("p (a r) -> p a r", a=PASSES),
                 wt_scales[:, 4 * q : 4 * q + 4, :].bitcast(I32).rearrange("a p r -> p a r"),
             )
-        nc.sync.dma_start(ws_raw[1][:], ws_rows[1])
-        wt_raw = sb("wt_raw", [P, PASSES, R], I32)
-        nc.sync.dma_start(wt_raw[:], wt_words.rearrange("a p r b -> p a (r b)").bitcast(I32))
+        for c in range(2):
+            nc.sync.dma_start(ws_raw[1][:, :, c * WIDE : (c + 1) * WIDE], ws_rows[1][:, :, c * WIDE : (c + 1) * WIDE])
 
         picked_sc = sb("picked_sc", [P, 2 * J], U8)
         for side in range(2):
@@ -81,16 +97,8 @@ def tile_list_msg_gelu_gate_kernel(
                 picked_sc[96 + 8 * q : 96 + 8 * q + 8, :].bitcast(I32),
             )
 
-        wd_raw = at("wd_raw", [P, PACK, N], F32, 8192)
-        nc.sync.dma_start(wd_raw[:], wd.rearrange("(p t) n -> p t n", t=PACK))
-
-        def round_ws(a):
-            grouped = at("ws_bf%d" % a, [P, R * PACK], BF16, (43008, 53312)[a])
-            nc.scalar.copy(
-                grouped[:].rearrange("p (t m i) -> p m i t", t=PACK, i=PACK),
-                ws_raw[a][:].rearrange("p i (m t) -> p m i t", t=PACK),
-            )
-            return grouped
+        def interleave(grouped, planes):
+            nc.scalar.copy(grouped.rearrange("p (j c t) -> p j t c", t=PACK, c=LINE), planes.rearrange("p t (j c) -> p j t c", c=LINE))
 
         def quantise(name, grouped, width, offset=None):
             codes = sb(name + "_codes", [P, width], U32) if offset is None else at(name + "_codes", [P, width], U32, offset)
@@ -98,127 +106,128 @@ def tile_list_msg_gelu_gate_kernel(
             nc.vector.quantize_mx(out=codes[:].bitcast(FP8X4), scales=scales[:], in_=grouped)
             return codes, scales
 
-        def pick_words(h, picked):
-            for side in range(2):
-                nc.vector.tensor_copy(picked[side][:], tab_w[:].bitcast(U32).indirect(lists[side][:, h * COLS : (h + 1) * COLS]))
+        def pick_words(picked, h, side):
+            nc.vector.tensor_copy(picked[:], tab_w[:].bitcast(U32).indirect(lists[side][:, h * COLS : (h + 1) * COLS]))
 
-        def part_words(h, picked):
-            parted = []
-            for side in range(2):
-                parted.append(sb("parted%d%d" % (h, side), [P, PASSES * HALF * 2], U8))
-                nc.vector.tensor_copy(
-                    parted[side][:].bitcast(U16).rearrange("p (a j) -> p a j", a=PASSES),
-                    picked[side][:].bitcast(U16).rearrange("p (j a) -> p a j", a=PASSES),
-                )
-            return parted
+        def part_words(parted, picked):
+            nc.vector.tensor_copy(
+                parted[:].bitcast(U16).rearrange("p (a j) -> p a j", a=PASSES),
+                picked[:].bitcast(U16).rearrange("p (j a) -> p a j", a=PASSES),
+            )
 
-        ws_bf = [round_ws(a) for a in range(PASSES)]
-        ws_q = [quantise("ws0", ws_bf[0][:], R)]
-        picked = [sb("picked_w0%d" % side, [P, HALF], U32) for side in range(2)]
-        pick_words(0, picked)
-        parted = [part_words(0, picked)]
-        wt_codes = sb("wt_codes", [P, PASSES, R], I32)
-        wt_sc = sb("wt_sc", [P, PASSES * R], U8)
-        nc.vector.tensor_copy(
-            wt_sc[:].rearrange("p (a t m) -> p a t m", a=PASSES, t=PACK),
-            wt_sc_raw[:].rearrange("p (a m t) -> p a t m", a=PASSES, t=PACK),
-        )
-        nc.scalar.copy(
-            wt_codes[:].bitcast(U32).rearrange("p a (t m) -> p a m t", t=PACK),
-            wt_raw[:].bitcast(U32).rearrange("p a (m t) -> p a m t", t=PACK),
-        )
-        ws_q.append(quantise("ws1", ws_bf[1][:], R))
-        picked = [at("picked_w1%d" % side, [P, HALF], U32, side * HALF * 4) for side in range(2)]
-        pick_words(1, picked)
-        parted.append(part_words(1, picked))
+        ws_bf = [at("ws_bf0", [P, R * PACK], BF16, ws_bf0_at), at("ws_bf1", [P, R * PACK], BF16, ws_bf1_at)]
+        interleave(ws_bf[0][:], ws_raw[0][:])
+        for c in range(2):
+            interleave(ws_bf[1][:, c * WIDE * PACK : (c + 1) * WIDE * PACK], ws_raw[1][:, :, c * WIDE : (c + 1) * WIDE])
 
-        gates = [at("gates%d" % n, [P, T], F32, offset) for n, offset in enumerate((45120, 16384, 28736, 36928))]
-        wgo_sb = at("wgo_sb", [P, J], F32, 24576)
-        nc.sync.dma_start(gates[1][:], gT[P : 2 * P, :])
+        wt_codes = at("wt_codes", [P, PASSES, R], I32, wt_codes_at)
+        nc.sync.dma_start(wt_codes[:], wt_words.rearrange("a p r b -> p a (r b)").bitcast(I32))
+        wgo_sb = at("wgo_sb", [P, J], F32, 0)
+        sm_sb = at("sm_sb", [P, PACK], F32, tab_sc_at + LAP)
+        gates = {
+            1: at("gates1", [P, T], F32, ws_raw0_at + LAP - PAGE_BYTES),
+            2: at("gates2", [P, T], F32, gates2_at),
+            3: at("gates3", [P, T], F32, ws_bf0_at + LAP - PAGE_BYTES),
+            0: at("gates0", [P, T], F32, ws_bf1_at + LAP - PAGE_BYTES),
+        }
+        wd_raw = [at("wd_raw%d" % c, [P, PACK, WIDE], F32, offset) for c, offset in enumerate((wd_raw0_at, wd_raw1_at))]
+        wd_rows = wd.rearrange("(p t) n -> p t n", t=PACK)
         nc.sync.dma_start(wgo_sb[:], wgo)
-        sm_sb = at("sm_sb", [P, PACK], F32, 28672)
         nc.sync.dma_start(sm_sb[:], sm.rearrange("(p t) -> p t", t=PACK))
-        for n in (2, 3, 0):
+        for n in range(1, PAGES):
             nc.sync.dma_start(gates[n][:], gT[n * P : (n + 1) * P, :])
+        nc.sync.dma_start(wd_raw[0][:], wd_rows[:, :, 0:WIDE])
+        nc.sync.dma_start(gates[0][:], gT[0:P, :])
+        nc.sync.dma_start(wd_raw[1][:], wd_rows[:, :, WIDE:N])
 
-        wd_bf = sb("wd_bf", [P, N * PACK], BF16)
-        nc.scalar.copy(wd_bf[:].rearrange("p (n c t) -> p n t c", t=PACK, c=LINE), wd_raw[:].rearrange("p t (n c) -> p n t c", c=LINE))
-        wd_codes, wd_sc = quantise("wd", wd_bf[:], N)
+        picked = [
+            [sb("picked00", [P, HALF], U32), at("picked01", [P, HALF], U32, ws_raw0_at + LAP)],
+            [at("picked1%d" % side, [P, HALF], U32, ws_raw1_at + (side + 1) * words) for side in range(2)],
+        ]
+        parted = [
+            [at("parted00", [P, words], U8, ws_raw0_at + LAP + words), at("parted01", [P, words], U8, ws_raw1_at)],
+            [sb("parted1%d" % side, [P, words], U8) for side in range(2)],
+        ]
+        ws_q = []
+        pick_words(picked[0][0], 0, 0)
+        ws_q.append(quantise("ws0", ws_bf[0][:], R))
+        part_words(parted[0][0], picked[0][0])
+        pick_words(picked[0][1], 0, 1)
+        ws_q.append(quantise("ws1", ws_bf[1][:], R))
+        part_words(parted[0][1], picked[0][1])
+        for side in range(2):
+            pick_words(picked[1][side], 1, side)
+        for side in range(2):
+            part_words(parted[1][side], picked[1][side])
+        windows = [at("window0", [P, T], F32, ws_raw1_at + words)]
+        nc.gpsimd.memset(windows[0][:].bitcast(I32), 0)
 
-        def first_product(h):
-            banks = [psum.tile([P, 2, PART], F32, name="a%d%d" % (h, b), tag="bank%d" % (PACK * h + b)) for b in range(PACK)]
+        def activate(b, act):
+            h, first = divmod(b * P, HALF)
+            bank = psum.tile([P, R], F32, name="sum%d" % b, tag="bank%d" % b)
             order = [(0, 0), (0, 1), (1, 0), (1, 1)]
-            steps = [(b, e, 0) for b in range(2) for e in range(2)]
-            steps = steps + [(b, e, step) for b in range(PACK) for step in range(len(order)) for e in range(2) if b > 1 or step > 0]
-            for b, e, step in steps:
-                side, a = order[step]
-                t = 2 * (b % 2) + e
-                cols = slice(t * P, (t + 1) * P)
+            for step, (side, a) in enumerate(order):
                 if side == 0:
-                    w_codes, w_sc = ws_q[a][0][:, cols], ws_q[a][1][:, cols]
+                    w_codes, w_sc = ws_q[a][0][:], ws_q[a][1][:]
                 else:
-                    w_codes = wt_codes[:, a, cols]
-                    w_sc = wt_sc[:, a * R + t * P : a * R + (t + 1) * P]
-                first = (b // 2) * PART
-                words = a * HALF + first
-                edges = (2 * a + side) * J + h * HALF + first
+                    w_codes, w_sc = wt_codes[:, a, :], wt_sc[:, a * R : (a + 1) * R]
+                word = a * HALF + first
+                edge = (2 * a + side) * J + b * P
                 nc.tensor.matmul_mx(
-                    out=banks[b][:, e, :],
-                    lhsT=w_codes.bitcast(FP8X4),
-                    lhsT_scale=w_sc,
-                    rhs=parted[h][side][:, 2 * words : 2 * (words + PART)].bitcast(FP4X4),
-                    rhs_scale=tab_planes[:, edges : edges + PART],
-                    start=(step == 0 and e == 0),
-                    stop=(step == len(order) - 1 and e == 1),
+                    out=bank[:],
+                    lhsT=parted[h][side][:, 2 * word : 2 * (word + P)].bitcast(FP4X4),
+                    lhsT_scale=tab_planes[:, edge : edge + P],
+                    rhs=w_codes.bitcast(FP8X4),
+                    rhs_scale=w_sc,
+                    start=(step == 0),
+                    stop=(step == len(order) - 1),
                 )
-            return banks
+            nc.scalar.activation(act, bank[:].rearrange("p (m t) -> p t m", t=PACK), ACT.Gelu_apprx_tanh)
 
-        def hidden(h, banks):
-            act = at("act%d" % h, [P, 2, PACK, PART], F32, 8192)
-            rounded = sb("rounded%d" % h, [P, 2, PACK, PART], BF16, tag=("rounded0", "h_bf0")[h])
+        def hidden(h, act, rounded):
             grouped = sb("h_bf%d" % h, [P, 2, PART * PACK], BF16)
-            for q in range(2):
-                for pair in range(2):
-                    nc.scalar.activation(act[:, q, 2 * pair : 2 * pair + 2, :], banks[2 * q + pair][:], ACT.Gelu_apprx_tanh)
+            turned = [psum.tile([P, 2, PART], F32, name="turned%d%d" % (h, u), tag="bank%d" % (PACK * (1 - h) + u)) for u in range(PACK)]
+            for b in range(PACK):
+                activate(PACK * h + b, act[:, b])
+            for b in range(PACK):
                 for t in range(PACK):
-                    nc.scalar.activation(rounded[:, q, t, :], act[:, q, t, :], ACT.Copy, scale=sm_sb[:, t : t + 1])
-                nc.scalar.copy(
-                    grouped[:, q, :].rearrange("p (j c t) -> p j t c", t=PACK, c=LINE),
-                    rounded[:, q].rearrange("p t (j c) -> p j t c", c=LINE),
-                )
+                    nc.tensor.transpose(turned[2 * (b // 2) + t // 2][:, t % 2, (b % 2) * P : (b % 2 + 1) * P], act[:, b, t, :], ident[:])
+            for q in range(2):
+                for t in range(PACK):
+                    nc.scalar.activation(rounded[:, q, t, :], turned[2 * q + t // 2][:, t % 2, :], ACT.Copy, scale=sm_sb[:, t : t + 1])
+                interleave(grouped[:, q, :], rounded[:, q])
             return grouped[:].rearrange("p q w -> p (q w)")
 
-        def message(h, n, h_codes, h_sc, msg):
+        def quantise_wd(c, offset):
+            grouped = at("wd_bf%d" % c, [P, WIDE * PACK], BF16, offset)
+            interleave(grouped[:], wd_raw[c][:])
+            return quantise("wd%d" % c, grouped[:], WIDE)
+
+        def place(h, n, msg):
             bank = psum.tile([P, HALF], F32, name="y%d%d" % (h, n), tag="bank%d" % (PACK * h + n))
+            wd_codes, wd_sc = wd_q[n // 2]
+            cols = slice((n % 2) * P, (n % 2 + 1) * P)
             nc.tensor.matmul_mx(
                 out=bank[:],
-                lhsT=wd_codes[:, n * P : (n + 1) * P].bitcast(FP8X4),
-                lhsT_scale=wd_sc[:, n * P : (n + 1) * P],
-                rhs=h_codes[:].bitcast(FP8X4),
-                rhs_scale=h_sc[:],
+                lhsT=wd_codes[:, cols].bitcast(FP8X4),
+                lhsT_scale=wd_sc[:, cols],
+                rhs=h_q[h][0][:].bitcast(FP8X4),
+                rhs_scale=h_q[h][1][:],
                 start=True,
                 stop=True,
             )
-            nc.scalar.copy(msg, bank[:])
-
-        sums = [first_product(h) for h in range(HALVES)]
-
-        def weigh_gates(n, tag=None):
-            held = sb("gate_w%d" % n, [P, J], F32, tag=tag)
-            nc.vector.tensor_tensor(held[:], gates[n][:].indirect(lists[0][:]), wgo_sb[:], MULT)
-            return held
-
-        def place(h, n, h_codes, h_sc, tag=None):
-            msg = sb("msg%d%d" % (h, n), [P, HALF], F32, tag=tag)
-            message(h, n, h_codes, h_sc, msg[:])
+            nc.scalar.copy(msg[:], bank[:])
             nc.vector.tensor_tensor(
                 windows[n][:].indirect(lists[1][:, h * COLS : (h + 1) * COLS]), msg[:], weighted[n][:, h * HALF : (h + 1) * HALF], MULT
             )
 
-        last = PAGES - 1
-        weighted = [None] + [weigh_gates(n) for n in range(1, PAGES)]
-        h_q = [quantise("h0", hidden(0, sums[0]), HALF, 36928)]
-        weighted[0] = sb("gate_w0", [P, J], F32, tag="rounded0")
+        weighted = {}
+        for n in range(1, PAGES):
+            weighted[n] = sb("gate_w%d" % n, [P, J], F32)
+            nc.vector.tensor_tensor(weighted[n][:], gates[n][:].indirect(lists[0][:]), wgo_sb[:], MULT)
+        h_q = [quantise("h0", hidden(0, sb("act0", [P, PACK, PACK, P], F32), at("rounded0", [P, 2, PACK, PART], BF16, rounded0_at)), HALF, gates2_at + PAGE_BYTES + LAP - words)]
+        wd_q = [quantise_wd(0, rounded0_at)]
+        weighted[0] = at("gate_w0", [P, J], F32, wd_raw0_at + LAP)
         for h in range(HALVES):
             nc.vector.tensor_tensor(
                 weighted[0][:, h * HALF : (h + 1) * HALF],
@@ -226,18 +235,17 @@ def tile_list_msg_gelu_gate_kernel(
                 wgo_sb[:, h * HALF : (h + 1) * HALF],
                 MULT,
             )
-        for n, offset in ((1, 16384), (2, 45120)):
+        for n, offset in ((1, rounded0_at + LAP - PAGE_BYTES), (2, rounded0_at + LAP)):
             windows.append(at("window%d" % n, [P, T], F32, offset))
             nc.gpsimd.memset(windows[n][:].bitcast(I32), 0)
-        for n in range(last - 1):
-            place(0, n, *h_q[0])
-        h_q.append(quantise("h1", hidden(1, sums[1]), HALF))
-        place(0, last - 1, *h_q[0], tag="h_bf0")
-        for n in range(last):
-            place(1, n, *h_q[1])
+        place(0, 0, sb("msg00", [P, HALF], F32))
+        wd_q.append(quantise_wd(1, wd_bf1_at))
+        windows.append(at("window3", [P, T], F32, wd_bf1_at))
+        nc.gpsimd.memset(windows[3][:].bitcast(I32), 0)
+        place(0, 1, at("msg01", [P, HALF], F32, wd_raw1_at))
+        place(0, 2, sb("msg02", [P, HALF], F32))
+        h_q.append(quantise("h1", hidden(1, at("act1", [P, PACK, PACK, P], F32, wd_raw0_at + LAP - PAGE_BYTES), sb("rounded1", [P, 2, PACK, PART], BF16)), HALF))
+        place(0, 3, sb("msg03", [P, HALF], F32, tag="rounded1"))
+        for n in range(PAGES):
+            place(1, n, sb("msg1%d" % n, [P, HALF], F32))
             nc.sync.dma_start(out[n * P : (n + 1) * P, :], windows[n][:])
-        msg = sb("msg_last", [P, J], F32)
-        for h in range(HALVES):
-            message(h, last, *h_q[h], msg[:, h * HALF : (h + 1) * HALF])
-        nc.vector.tensor_tensor(windows[0][:].indirect(lists[1][:]), msg[:], weighted[last][:], MULT)
-        nc.sync.dma_start(out[last * P : (last + 1) * P, :], windows[0][:])

@@ -30,6 +30,7 @@ PAGES = N // P
 WIDE = N // 2
 PAGE_BYTES = T * 4
 LAP = 64
+DEALT = J // P
 
 
 def tile_list_msg_gelu_gate_kernel(
@@ -48,8 +49,8 @@ def tile_list_msg_gelu_gate_kernel(
             return laid.tile(shape, dtype, name=name, tag=name, align_bytes=64, offset=offset)
 
         words = HALF * 4
-        tab_sc_at = J * 4 - LAP
-        wt_codes_at = tab_sc_at + 2 * LAP
+        tab_sc_at = 0
+        wt_codes_at = tab_sc_at + LAP
         ws_raw0_at = wt_codes_at + PASSES * R * 4 + PAGE_BYTES - LAP
         gates2_at = ws_raw0_at + LAP + 2 * words
         ws_bf0_at = gates2_at + 2 * PAGE_BYTES - LAP
@@ -74,6 +75,8 @@ def tile_list_msg_gelu_gate_kernel(
         nc.sync.dma_start(lists[0][:], offs)
         nc.sync.dma_start(tab_sc[96:P, :].bitcast(I32), tab_scales.rearrange("a q t -> q a t").bitcast(I32))
         nc.sync.dma_start(lists[1][:], offs2)
+        wgo_dealt = sb("wgo_dealt", [P, DEALT], F32)
+        nc.sync.dma_start(wgo_dealt[:], wgo[0].rearrange("(p m) -> p m", m=DEALT))
 
         ws_raw = [at("ws_raw0", [P, PACK, R], F32, ws_raw0_at), at("ws_raw1", [P, PACK, R], F32, ws_raw1_at)]
         ws_rows = ws.rearrange("(a p i) r -> a p i r", a=PASSES, i=PACK)
@@ -115,6 +118,16 @@ def tile_list_msg_gelu_gate_kernel(
                 picked[:].bitcast(U16).rearrange("p (j a) -> p a j", a=PASSES),
             )
 
+        wgo_sb = sb("wgo_sb", [P, J], F32)
+        for u in range(DEALT // LINE):
+            spread = psum.tile([P, LINE, P], F32, name="spread%d" % u, tag="bank%d" % u)
+            for m in range(LINE):
+                column = wgo_dealt[:, LINE * u + m : LINE * u + m + 1]
+                nc.tensor.transpose(spread[:, m, :], column.to_broadcast([P, P]), ident[:])
+            nc.scalar.copy(
+                wgo_sb[:].rearrange("p (n m) -> p n m", m=DEALT)[:, :, LINE * u : LINE * (u + 1)], spread[:].rearrange("p m n -> p n m")
+            )
+
         ws_bf = [at("ws_bf0", [P, R * PACK], BF16, ws_bf0_at), at("ws_bf1", [P, R * PACK], BF16, ws_bf1_at)]
         interleave(ws_bf[0][:], ws_raw[0][:])
         for c in range(2):
@@ -122,8 +135,7 @@ def tile_list_msg_gelu_gate_kernel(
 
         wt_codes = at("wt_codes", [P, PASSES, R], I32, wt_codes_at)
         nc.sync.dma_start(wt_codes[:], wt_words.rearrange("a p r b -> p a (r b)").bitcast(I32))
-        wgo_sb = at("wgo_sb", [P, J], F32, 0)
-        sm_sb = at("sm_sb", [P, PACK], F32, tab_sc_at + LAP)
+        sm_sb = at("sm_sb", [P, PACK], F32, tab_sc_at)
         gates = {
             1: at("gates1", [P, T], F32, ws_raw0_at + LAP - PAGE_BYTES),
             2: at("gates2", [P, T], F32, gates2_at),
@@ -132,7 +144,6 @@ def tile_list_msg_gelu_gate_kernel(
         }
         wd_raw = [at("wd_raw%d" % c, [P, PACK, WIDE], F32, offset) for c, offset in enumerate((wd_raw0_at, wd_raw1_at))]
         wd_rows = wd.rearrange("(p t) n -> p t n", t=PACK)
-        nc.sync.dma_start(wgo_sb[:], wgo)
         nc.sync.dma_start(sm_sb[:], sm.rearrange("(p t) -> p t", t=PACK))
         for n in range(1, PAGES):
             nc.sync.dma_start(gates[n][:], gT[n * P : (n + 1) * P, :])

@@ -49,17 +49,19 @@ def tile_list_msg_gelu_gate_kernel(
             return laid.tile(shape, dtype, name=name, tag=name, align_bytes=64, offset=offset)
 
         words = HALF * 4
-        tab_sc_at = 0
-        wt_codes_at = tab_sc_at + LAP
-        ws_raw0_at = wt_codes_at + PASSES * R * 4 + PAGE_BYTES - LAP
+        wt_codes_at = 0
+        tab_sc_at = wt_codes_at + PASSES * R * 4 - LAP
+        wd_raw0_at = tab_sc_at + 2 * LAP
+        ws_raw0_at = wd_raw0_at + WIDE * PACK * 4 + PAGE_BYTES - LAP
         gates2_at = ws_raw0_at + LAP + 2 * words
-        ws_bf0_at = gates2_at + 2 * PAGE_BYTES - LAP
-        wd_raw0_at = ws_bf0_at + LAP
-        ws_bf1_at = wd_raw0_at + WIDE * PACK * 4 + PAGE_BYTES
+        gates3_at = gates2_at + PAGE_BYTES
+        ws_bf0_at = gates3_at + PAGE_BYTES - LAP
+        ws_bf1_at = ws_bf0_at + R * PACK * 2 + PAGE_BYTES - LAP
         wd_raw1_at = ws_bf1_at + LAP
         ws_raw1_at = wd_raw1_at + WIDE * PACK * 4
         rounded0_at = ws_raw1_at + words + 2 * PAGE_BYTES - LAP
-        wd_bf1_at = rounded0_at + LAP + PAGE_BYTES
+        h_bf0_at = rounded0_at + J * 4 + PAGE_BYTES
+        wd_bf1_at = h_bf0_at + LAP + PAGE_BYTES
 
         lists = [keep.tile([P, J // 16], U16, name="src_list"), keep.tile([P, J // 16], U16, name="dst_list")]
         tab_sc = at("tab_sc", [P, T], U8, tab_sc_at)
@@ -67,9 +69,9 @@ def tile_list_msg_gelu_gate_kernel(
         tab_planes = sb("tab_planes", [P, PASSES * 2 * J], U8)
         ident = sb("ident", [P, P], F32)
 
-        nc.gpsimd.memset(wt_sc[:].bitcast(I32), 0)
-        nc.gpsimd.memset(tab_sc[0:96, :].bitcast(I32), 0)
         make_identity(nc, ident[:])
+        nc.vector.memset(wt_sc[:].bitcast(I32), 0)
+        nc.vector.memset(tab_sc[0:96, :].bitcast(I32), 0)
         nc.vector.memset(tab_planes[:].bitcast(I32), 0)
 
         nc.sync.dma_start(lists[0][:], offs)
@@ -135,19 +137,19 @@ def tile_list_msg_gelu_gate_kernel(
 
         wt_codes = at("wt_codes", [P, PASSES, R], I32, wt_codes_at)
         nc.sync.dma_start(wt_codes[:], wt_words.rearrange("a p r b -> p a (r b)").bitcast(I32))
-        sm_sb = at("sm_sb", [P, PACK], F32, tab_sc_at)
+        sm_sb = at("sm_sb", [P, PACK], F32, tab_sc_at + LAP)
         gates = {
             1: at("gates1", [P, T], F32, ws_raw0_at + LAP - PAGE_BYTES),
             2: at("gates2", [P, T], F32, gates2_at),
-            3: at("gates3", [P, T], F32, ws_bf0_at + LAP - PAGE_BYTES),
+            3: at("gates3", [P, T], F32, gates3_at),
             0: at("gates0", [P, T], F32, ws_bf1_at + LAP - PAGE_BYTES),
         }
         wd_raw = [at("wd_raw%d" % c, [P, PACK, WIDE], F32, offset) for c, offset in enumerate((wd_raw0_at, wd_raw1_at))]
         wd_rows = wd.rearrange("(p t) n -> p t n", t=PACK)
         nc.sync.dma_start(sm_sb[:], sm.rearrange("(p t) -> p t", t=PACK))
+        nc.sync.dma_start(wd_raw[0][:], wd_rows[:, :, 0:WIDE])
         for n in range(1, PAGES):
             nc.sync.dma_start(gates[n][:], gT[n * P : (n + 1) * P, :])
-        nc.sync.dma_start(wd_raw[0][:], wd_rows[:, :, 0:WIDE])
         nc.sync.dma_start(gates[0][:], gT[0:P, :])
         nc.sync.dma_start(wd_raw[1][:], wd_rows[:, :, WIDE:N])
 
@@ -195,27 +197,19 @@ def tile_list_msg_gelu_gate_kernel(
                 )
             nc.scalar.activation(act, bank[:].rearrange("p (m t) -> p t m", t=PACK), ACT.Gelu_apprx_tanh)
 
-        def hidden(h, act, rounded):
-            grouped = sb("h_bf%d" % h, [P, 2, PART * PACK], BF16)
-            turned = [psum.tile([P, 2, PART], F32, name="turned%d%d" % (h, u), tag="bank%d" % (PACK * (1 - h) + u)) for u in range(PACK)]
-            for b in range(PACK):
-                activate(PACK * h + b, act[:, b])
-            for b in range(PACK):
-                for t in range(PACK):
-                    nc.tensor.transpose(turned[2 * (b // 2) + t // 2][:, t % 2, (b % 2) * P : (b % 2 + 1) * P], act[:, b, t, :], ident[:])
+        def hidden(h, act, rounded, grouped):
+            turned = [psum.tile([P, 2, PART], F32, name="turned%d%d" % (h, u), tag="bank%d" % (PACK + u if h == 0 else 2 + u % 2)) for u in range(PACK)]
             for q in range(2):
+                for e in range(2):
+                    for t in range(PACK):
+                        nc.tensor.transpose(turned[2 * q + t // 2][:, t % 2, e * P : (e + 1) * P], act[:, 2 * q + e, t, :], ident[:])
                 for t in range(PACK):
                     nc.scalar.activation(rounded[:, q, t, :], turned[2 * q + t // 2][:, t % 2, :], ACT.Copy, scale=sm_sb[:, t : t + 1])
                 interleave(grouped[:, q, :], rounded[:, q])
             return grouped[:].rearrange("p q w -> p (q w)")
 
-        def quantise_wd(c, offset):
-            grouped = at("wd_bf%d" % c, [P, WIDE * PACK], BF16, offset)
-            interleave(grouped[:], wd_raw[c][:])
-            return quantise("wd%d" % c, grouped[:], WIDE)
-
         def place(h, n, msg):
-            bank = psum.tile([P, HALF], F32, name="y%d%d" % (h, n), tag="bank%d" % (PACK * h + n))
+            bank = psum.tile([P, HALF], F32, name="y%d%d" % (h, n), tag="bank%d" % (n % 2 if h == 0 else PACK + n))
             wd_codes, wd_sc = wd_q[n // 2]
             cols = slice((n % 2) * P, (n % 2 + 1) * P)
             nc.tensor.matmul_mx(
@@ -236,9 +230,16 @@ def tile_list_msg_gelu_gate_kernel(
         for n in range(1, PAGES):
             weighted[n] = sb("gate_w%d" % n, [P, J], F32)
             nc.vector.tensor_tensor(weighted[n][:], gates[n][:].indirect(lists[0][:]), wgo_sb[:], MULT)
-        h_q = [quantise("h0", hidden(0, sb("act0", [P, PACK, PACK, P], F32), at("rounded0", [P, 2, PACK, PART], BF16, rounded0_at)), HALF, gates2_at + PAGE_BYTES + LAP - words)]
-        wd_q = [quantise_wd(0, rounded0_at)]
-        weighted[0] = at("gate_w0", [P, J], F32, wd_raw0_at + LAP)
+        act = sb("act0", [P, PACK, PACK, P], F32)
+        wd_bf = [sb("wd_bf0", [P, WIDE * PACK], BF16), at("wd_bf1", [P, WIDE * PACK], BF16, wd_bf1_at)]
+        activate(0, act[:, 0])
+        interleave(wd_bf[0][:], wd_raw[0][:])
+        for b in range(1, PACK):
+            activate(b, act[:, b])
+        h_bf = hidden(0, act, at("rounded0", [P, 2, PACK, PART], BF16, rounded0_at), at("h_bf0", [P, 2, PART * PACK], BF16, h_bf0_at))
+        wd_q = [quantise("wd0", wd_bf[0][:], WIDE, gates3_at + LAP)]
+        h_q = [quantise("h0", h_bf, HALF, gates3_at + LAP - words)]
+        weighted[0] = at("gate_w0", [P, J], F32, rounded0_at + LAP)
         for h in range(HALVES):
             nc.vector.tensor_tensor(
                 weighted[0][:, h * HALF : (h + 1) * HALF],
@@ -246,16 +247,21 @@ def tile_list_msg_gelu_gate_kernel(
                 wgo_sb[:, h * HALF : (h + 1) * HALF],
                 MULT,
             )
-        for n, offset in ((1, rounded0_at + LAP - PAGE_BYTES), (2, rounded0_at + LAP)):
+        for n, offset in ((1, h_bf0_at + LAP - PAGE_BYTES), (2, h_bf0_at + LAP)):
             windows.append(at("window%d" % n, [P, T], F32, offset))
             nc.gpsimd.memset(windows[n][:].bitcast(I32), 0)
         place(0, 0, sb("msg00", [P, HALF], F32))
-        wd_q.append(quantise_wd(1, wd_bf1_at))
+        interleave(wd_bf[1][:], wd_raw[1][:])
+        wd_q.append(quantise("wd1", wd_bf[1][:], WIDE))
         windows.append(at("window3", [P, T], F32, wd_bf1_at))
         nc.gpsimd.memset(windows[3][:].bitcast(I32), 0)
         place(0, 1, at("msg01", [P, HALF], F32, wd_raw1_at))
         place(0, 2, sb("msg02", [P, HALF], F32))
-        h_q.append(quantise("h1", hidden(1, at("act1", [P, PACK, PACK, P], F32, wd_raw0_at + LAP - PAGE_BYTES), sb("rounded1", [P, 2, PACK, PART], BF16)), HALF))
+        act = at("act1", [P, PACK, PACK, P], F32, rounded0_at + LAP - PAGE_BYTES)
+        for b in range(PACK):
+            activate(PACK + b, act[:, b])
+        h_bf = hidden(1, act, sb("rounded1", [P, 2, PACK, PART], BF16), sb("h_bf1", [P, 2, PART * PACK], BF16))
+        h_q.append(quantise("h1", h_bf, HALF))
         place(0, 3, sb("msg03", [P, HALF], F32, tag="rounded1"))
         for n in range(PAGES):
             place(1, n, sb("msg1%d" % n, [P, HALF], F32))

@@ -53,13 +53,13 @@ def tile_list_msg_gelu_gate_kernel(
         tab_sc_at = wt_codes_at + PASSES * R * 4 - LAP
         wd_raw0_at = tab_sc_at + 2 * LAP
         ws_raw0_at = wd_raw0_at + WIDE * PACK * 4 + PAGE_BYTES - LAP
-        gates2_at = ws_raw0_at + LAP + 2 * words
+        gates2_at = ws_raw0_at + LAP + 3 * words
         gates3_at = gates2_at + PAGE_BYTES
         ws_bf0_at = gates3_at + PAGE_BYTES - LAP
         ws_bf1_at = ws_bf0_at + R * PACK * 2 + PAGE_BYTES - LAP
         wd_raw1_at = ws_bf1_at + LAP
         ws_raw1_at = wd_raw1_at + WIDE * PACK * 4
-        rounded0_at = ws_raw1_at + words + 2 * PAGE_BYTES - LAP
+        rounded0_at = ws_raw1_at + 2 * words + 2 * PAGE_BYTES - LAP
         h_bf0_at = rounded0_at + J * 4 + PAGE_BYTES
         wd_bf1_at = h_bf0_at + LAP + PAGE_BYTES
 
@@ -155,30 +155,30 @@ def tile_list_msg_gelu_gate_kernel(
 
         picked = [
             [sb("picked00", [P, HALF], U32), at("picked01", [P, HALF], U32, ws_raw0_at + LAP)],
-            [at("picked1%d" % side, [P, HALF], U32, ws_raw1_at + (side + 1) * words) for side in range(2)],
+            [at("picked10", [P, HALF], U32, ws_raw0_at + LAP + 2 * words), at("picked11", [P, HALF], U32, ws_raw1_at + 2 * words)],
         ]
         parted = [
-            [at("parted00", [P, words], U8, ws_raw0_at + LAP + words), at("parted01", [P, words], U8, ws_raw1_at)],
-            [sb("parted1%d" % side, [P, words], U8) for side in range(2)],
+            [at("parted00", [P, words], U8, ws_raw0_at + LAP + words), sb("parted01", [P, words], U8)],
+            [at("parted10", [P, words], U8, ws_raw1_at + words), sb("parted11", [P, words], U8)],
         ]
         ws_q = []
         pick_words(picked[0][0], 0, 0)
         ws_q.append(quantise("ws0", ws_bf[0][:], R))
         part_words(parted[0][0], picked[0][0])
         pick_words(picked[0][1], 0, 1)
-        ws_q.append(quantise("ws1", ws_bf[1][:], R))
+        pick_words(picked[1][0], 1, 0)
         part_words(parted[0][1], picked[0][1])
-        for side in range(2):
-            pick_words(picked[1][side], 1, side)
+        ws_q.append(quantise("ws1", ws_bf[1][:], R))
+        pick_words(picked[1][1], 1, 1)
         for side in range(2):
             part_words(parted[1][side], picked[1][side])
-        windows = [at("window0", [P, T], F32, ws_raw1_at + words)]
+        windows = [at("window0", [P, T], F32, ws_raw1_at + 2 * words)]
         nc.gpsimd.memset(windows[0][:].bitcast(I32), 0)
 
         def activate(b, act):
             h, first = divmod(b * P, HALF)
             bank = psum.tile([P, R], F32, name="sum%d" % b, tag="bank%d" % b)
-            order = [(0, 0), (0, 1), (1, 0), (1, 1)]
+            order = [(0, 0), (1, 0), (1, 1), (0, 1)]
             for step, (side, a) in enumerate(order):
                 if side == 0:
                     w_codes, w_sc = ws_q[a][0][:], ws_q[a][1][:]

@@ -27,7 +27,8 @@ COLS = HALF // 16
 PART = 2 * P
 LINE = 4
 PAGES = N // P
-WIDE = N // 2
+WIDE = R // 2
+REST = N - P
 PAGE_BYTES = T * 4
 LAP = 64
 DEALT = J // P
@@ -51,17 +52,15 @@ def tile_list_msg_gelu_gate_kernel(
         words = HALF * 4
         wt_codes_at = 0
         tab_sc_at = wt_codes_at + PASSES * R * 4 - LAP
-        wd_raw0_at = tab_sc_at + 2 * LAP
-        ws_raw0_at = wd_raw0_at + WIDE * PACK * 4 + PAGE_BYTES - LAP
-        gates2_at = ws_raw0_at + LAP + 3 * words
-        gates3_at = gates2_at + PAGE_BYTES
-        ws_bf0_at = gates3_at + PAGE_BYTES - LAP
-        ws_bf1_at = ws_bf0_at + R * PACK * 2 + PAGE_BYTES - LAP
+        ws_raw0_at = tab_sc_at + T + PAGE_BYTES - LAP
+        wd_raw0_at = ws_raw0_at + LAP + 3 * words
+        ws_bf0_at = wd_raw0_at + P * PACK * 4 + PAGE_BYTES - LAP
+        gates2_at = ws_bf0_at + LAP
+        ws_bf1_at = gates2_at + 2 * PAGE_BYTES - LAP
         wd_raw1_at = ws_bf1_at + LAP
-        ws_raw1_at = wd_raw1_at + WIDE * PACK * 4
-        rounded0_at = ws_raw1_at + 2 * words + 2 * PAGE_BYTES - LAP
-        h_bf0_at = rounded0_at + J * 4 + PAGE_BYTES
-        wd_bf1_at = h_bf0_at + LAP + PAGE_BYTES
+        ws_raw1_at = wd_raw1_at + words + PAGE_BYTES
+        rounded0_at = ws_raw1_at + 2 * words + PAGE_BYTES
+        wd_bf1_at = rounded0_at + P * 4 + J * 4 + PAGE_BYTES - LAP
 
         lists = [keep.tile([P, J // 16], U16, name="src_list"), keep.tile([P, J // 16], U16, name="dst_list")]
         tab_sc = at("tab_sc", [P, T], U8, tab_sc_at)
@@ -75,10 +74,10 @@ def tile_list_msg_gelu_gate_kernel(
         nc.vector.memset(tab_planes[:].bitcast(I32), 0)
 
         nc.sync.dma_start(lists[0][:], offs)
-        nc.sync.dma_start(tab_sc[96:P, :].bitcast(I32), tab_scales.rearrange("a q t -> q a t").bitcast(I32))
+        nc.scalar.dma_start(tab_sc[96:P, :].bitcast(I32), tab_scales.rearrange("a q t -> q a t").bitcast(I32))
         nc.sync.dma_start(lists[1][:], offs2)
         wgo_dealt = sb("wgo_dealt", [P, DEALT], F32)
-        nc.sync.dma_start(wgo_dealt[:], wgo[0].rearrange("(p m) -> p m", m=DEALT))
+        nc.scalar.dma_start(wgo_dealt[:], wgo[0].rearrange("(p m) -> p m", m=DEALT))
 
         ws_raw = [at("ws_raw0", [P, PACK, R], F32, ws_raw0_at), at("ws_raw1", [P, PACK, R], F32, ws_raw1_at)]
         ws_rows = ws.rearrange("(a p i) r -> a p i r", a=PASSES, i=PACK)
@@ -139,19 +138,19 @@ def tile_list_msg_gelu_gate_kernel(
         nc.sync.dma_start(wt_codes[:], wt_words.rearrange("a p r b -> p a (r b)").bitcast(I32))
         sm_sb = at("sm_sb", [P, PACK], F32, tab_sc_at + LAP)
         gates = {
-            1: at("gates1", [P, T], F32, ws_raw0_at + LAP - PAGE_BYTES),
+            0: at("gates0", [P, T], F32, ws_raw0_at + LAP - PAGE_BYTES),
+            1: at("gates1", [P, T], F32, gates2_at - PAGE_BYTES),
             2: at("gates2", [P, T], F32, gates2_at),
-            3: at("gates3", [P, T], F32, gates3_at),
-            0: at("gates0", [P, T], F32, ws_bf1_at + LAP - PAGE_BYTES),
+            3: at("gates3", [P, T], F32, ws_bf1_at + LAP - PAGE_BYTES),
         }
-        wd_raw = [at("wd_raw%d" % c, [P, PACK, WIDE], F32, offset) for c, offset in enumerate((wd_raw0_at, wd_raw1_at))]
+        wd_raw = [at("wd_raw0", [P, PACK, P], F32, wd_raw0_at), at("wd_raw1", [P, PACK, REST], F32, wd_raw1_at)]
         wd_rows = wd.rearrange("(p t) n -> p t n", t=PACK)
         nc.sync.dma_start(sm_sb[:], sm.rearrange("(p t) -> p t", t=PACK))
-        nc.sync.dma_start(wd_raw[0][:], wd_rows[:, :, 0:WIDE])
+        nc.sync.dma_start(gates[0][:], gT[0:P, :])
+        nc.sync.dma_start(wd_raw[0][:], wd_rows[:, :, 0:P])
         for n in range(1, PAGES):
             nc.sync.dma_start(gates[n][:], gT[n * P : (n + 1) * P, :])
-        nc.sync.dma_start(gates[0][:], gT[0:P, :])
-        nc.sync.dma_start(wd_raw[1][:], wd_rows[:, :, WIDE:N])
+        nc.sync.dma_start(wd_raw[1][:], wd_rows[:, :, P:N])
 
         picked = [
             [sb("picked00", [P, HALF], U32), at("picked01", [P, HALF], U32, ws_raw0_at + LAP)],
@@ -210,8 +209,8 @@ def tile_list_msg_gelu_gate_kernel(
 
         def place(h, n, msg):
             bank = psum.tile([P, HALF], F32, name="y%d%d" % (h, n), tag="bank%d" % (n % 2 if h == 0 else PACK + n))
-            wd_codes, wd_sc = wd_q[n // 2]
-            cols = slice((n % 2) * P, (n % 2 + 1) * P)
+            wd_codes, wd_sc = wd_q[min(n, 1)]
+            cols = slice(max(n - 1, 0) * P, max(n, 1) * P)
             nc.tensor.matmul_mx(
                 out=bank[:],
                 lhsT=wd_codes[:, cols].bitcast(FP8X4),
@@ -226,38 +225,31 @@ def tile_list_msg_gelu_gate_kernel(
                 windows[n][:].indirect(lists[1][:, h * COLS : (h + 1) * COLS]), msg[:], weighted[n][:, h * HALF : (h + 1) * HALF], MULT
             )
 
-        weighted = {}
-        for n in range(1, PAGES):
-            weighted[n] = sb("gate_w%d" % n, [P, J], F32)
-            nc.vector.tensor_tensor(weighted[n][:], gates[n][:].indirect(lists[0][:]), wgo_sb[:], MULT)
+        def weigh(n, held):
+            nc.vector.tensor_tensor(held[:], gates[n][:].indirect(lists[0][:]), wgo_sb[:], MULT)
+            return held
+
+        weighted = [weigh(n, sb("gate_w%d" % n, [P, J], F32)) for n in range(PAGES - 1)]
         act = sb("act0", [P, PACK, PACK, P], F32)
-        wd_bf = [sb("wd_bf0", [P, WIDE * PACK], BF16), at("wd_bf1", [P, WIDE * PACK], BF16, wd_bf1_at)]
-        activate(0, act[:, 0])
-        interleave(wd_bf[0][:], wd_raw[0][:])
-        for b in range(1, PACK):
+        wd_bf = [sb("wd_bf0", [P, P * PACK], BF16), at("wd_bf1", [P, REST * PACK], BF16, wd_bf1_at)]
+        for b in range(PACK):
             activate(b, act[:, b])
-        h_bf = hidden(0, act, at("rounded0", [P, 2, PACK, PART], BF16, rounded0_at), at("h_bf0", [P, 2, PART * PACK], BF16, h_bf0_at))
-        wd_q = [quantise("wd0", wd_bf[0][:], WIDE, gates3_at + LAP)]
-        h_q = [quantise("h0", h_bf, HALF, gates3_at + LAP - words)]
-        weighted[0] = at("gate_w0", [P, J], F32, rounded0_at + LAP)
-        for h in range(HALVES):
-            nc.vector.tensor_tensor(
-                weighted[0][:, h * HALF : (h + 1) * HALF],
-                gates[0][:].indirect(lists[0][:, h * COLS : (h + 1) * COLS]),
-                wgo_sb[:, h * HALF : (h + 1) * HALF],
-                MULT,
-            )
-        for n, offset in ((1, h_bf0_at + LAP - PAGE_BYTES), (2, h_bf0_at + LAP)):
+        interleave(wd_bf[0][:], wd_raw[0][:])
+        h_bf = hidden(0, act, at("rounded0", [P, 2, PACK, PART], BF16, rounded0_at), sb("h_bf0", [P, 2, PART * PACK], BF16))
+        wd_q = [quantise("wd0", wd_bf[0][:], P, rounded0_at)]
+        h_q = [quantise("h0", h_bf, HALF)]
+        weighted.append(weigh(PAGES - 1, at("gate_w3", [P, J], F32, rounded0_at + P * 4)))
+        interleave(wd_bf[1][:], wd_raw[1][:])
+        wd_q.append(quantise("wd1", wd_bf[1][:], REST))
+        for n, offset in ((1, wd_bf1_at + LAP - PAGE_BYTES), (2, wd_bf1_at + LAP)):
             windows.append(at("window%d" % n, [P, T], F32, offset))
             nc.gpsimd.memset(windows[n][:].bitcast(I32), 0)
-        place(0, 0, sb("msg00", [P, HALF], F32))
-        interleave(wd_bf[1][:], wd_raw[1][:])
-        wd_q.append(quantise("wd1", wd_bf[1][:], WIDE))
-        windows.append(at("window3", [P, T], F32, wd_bf1_at))
+        place(0, 0, at("msg00", [P, HALF], F32, wd_raw1_at))
+        windows.append(at("window3", [P, T], F32, wd_raw1_at + LAP - PAGE_BYTES))
         nc.gpsimd.memset(windows[3][:].bitcast(I32), 0)
-        place(0, 1, at("msg01", [P, HALF], F32, wd_raw1_at))
-        place(0, 2, sb("msg02", [P, HALF], F32))
-        act = at("act1", [P, PACK, PACK, P], F32, rounded0_at + LAP - PAGE_BYTES)
+        for n in (1, 2):
+            place(0, n, sb("msg0%d" % n, [P, HALF], F32))
+        act = at("act1", [P, PACK, PACK, P], F32, wd_raw1_at + words)
         for b in range(PACK):
             activate(PACK + b, act[:, b])
         h_bf = hidden(1, act, sb("rounded1", [P, 2, PACK, PART], BF16), sb("h_bf1", [P, 2, PART * PACK], BF16))

@@ -28,7 +28,6 @@ PART = 2 * P
 LINE = 4
 PAGES = N // P
 WIDE = R // 2
-REST = N - P
 PAGE_BYTES = T * 4
 LAP = 64
 DEALT = J // P
@@ -53,14 +52,17 @@ def tile_list_msg_gelu_gate_kernel(
         wt_codes_at = 0
         tab_sc_at = wt_codes_at + PASSES * R * 4 - LAP
         ws_raw0_at = tab_sc_at + T + PAGE_BYTES - LAP
-        wd_raw0_at = ws_raw0_at + LAP + 3 * words
-        ws_bf0_at = wd_raw0_at + P * PACK * 4 + PAGE_BYTES - LAP
+        wd_raw1_at = ws_raw0_at + LAP + 2 * words
+        act1_at = wd_raw1_at + words
+        ws_bf0_at = act1_at + 2 * PAGE_BYTES - LAP
         gates2_at = ws_bf0_at + LAP
         ws_bf1_at = gates2_at + 2 * PAGE_BYTES - LAP
-        wd_raw1_at = ws_bf1_at + LAP
-        ws_raw1_at = wd_raw1_at + words + PAGE_BYTES
-        rounded0_at = ws_raw1_at + 2 * words + PAGE_BYTES
-        wd_bf1_at = rounded0_at + P * 4 + J * 4 + PAGE_BYTES - LAP
+        wd_raw0_at = ws_bf1_at + LAP
+        wd_bf1_at = wd_raw0_at + 2 * words
+        rounded01_at = wd_bf1_at - LAP
+        window3_at = wd_bf1_at + words - LAP
+        ws_raw1_at = window3_at + PAGE_BYTES
+        window2_at = ws_raw1_at + 2 * words + PAGE_BYTES
 
         lists = [keep.tile([P, J // 16], U16, name="src_list"), keep.tile([P, J // 16], U16, name="dst_list")]
         tab_sc = at("tab_sc", [P, T], U8, tab_sc_at)
@@ -104,8 +106,8 @@ def tile_list_msg_gelu_gate_kernel(
         def interleave(grouped, planes):
             nc.scalar.copy(grouped.rearrange("p (j c t) -> p j t c", t=PACK, c=LINE), planes.rearrange("p t (j c) -> p j t c", c=LINE))
 
-        def quantise(name, grouped, width, offset=None):
-            codes = sb(name + "_codes", [P, width], U32) if offset is None else at(name + "_codes", [P, width], U32, offset)
+        def quantise(name, grouped, width):
+            codes = sb(name + "_codes", [P, width], U32)
             scales = sb(name + "_sc", [P, width], U8)
             nc.vector.quantize_mx(out=codes[:].bitcast(FP8X4), scales=scales[:], in_=grouped)
             return codes, scales
@@ -143,14 +145,13 @@ def tile_list_msg_gelu_gate_kernel(
             2: at("gates2", [P, T], F32, gates2_at),
             3: at("gates3", [P, T], F32, ws_bf1_at + LAP - PAGE_BYTES),
         }
-        wd_raw = [at("wd_raw0", [P, PACK, P], F32, wd_raw0_at), at("wd_raw1", [P, PACK, REST], F32, wd_raw1_at)]
+        wd_raw = [at("wd_raw%d" % c, [P, PACK, PART], F32, offset) for c, offset in enumerate((wd_raw0_at, wd_raw1_at))]
         wd_rows = wd.rearrange("(p t) n -> p t n", t=PACK)
         nc.sync.dma_start(sm_sb[:], sm.rearrange("(p t) -> p t", t=PACK))
-        nc.sync.dma_start(gates[0][:], gT[0:P, :])
-        nc.sync.dma_start(wd_raw[0][:], wd_rows[:, :, 0:P])
-        for n in range(1, PAGES):
+        for n in range(PAGES - 1):
             nc.sync.dma_start(gates[n][:], gT[n * P : (n + 1) * P, :])
-        nc.sync.dma_start(wd_raw[1][:], wd_rows[:, :, P:N])
+        nc.sync.dma_start(wd_raw[0][:], wd_rows[:, :, 0:PART])
+        nc.sync.dma_start(gates[PAGES - 1][:], gT[N - P : N, :])
 
         picked = [
             [sb("picked00", [P, HALF], U32), at("picked01", [P, HALF], U32, ws_raw0_at + LAP)],
@@ -171,12 +172,15 @@ def tile_list_msg_gelu_gate_kernel(
         pick_words(picked[1][1], 1, 1)
         for side in range(2):
             part_words(parted[1][side], picked[1][side])
+        nc.sync.dma_start(wd_raw[1][:], wd_rows[:, :, PART:N])
         windows = [at("window0", [P, T], F32, ws_raw1_at + 2 * words)]
         nc.gpsimd.memset(windows[0][:].bitcast(I32), 0)
+        sum_banks = (0, 1, 2, 3, 2, 3, 4, 5)
+        turn_banks = ((4, 5, 6, 7), (6, 7, 6, 7))
 
         def activate(b, act):
             h, first = divmod(b * P, HALF)
-            bank = psum.tile([P, R], F32, name="sum%d" % b, tag="bank%d" % b)
+            bank = psum.tile([P, R], F32, name="sum%d" % b, tag="bank%d" % sum_banks[b])
             order = [(0, 0), (1, 0), (1, 1), (0, 1)]
             for step, (side, a) in enumerate(order):
                 if side == 0:
@@ -196,65 +200,92 @@ def tile_list_msg_gelu_gate_kernel(
                 )
             nc.scalar.activation(act, bank[:].rearrange("p (m t) -> p t m", t=PACK), ACT.Gelu_apprx_tanh)
 
-        def hidden(h, act, rounded, grouped):
-            turned = [psum.tile([P, 2, PART], F32, name="turned%d%d" % (h, u), tag="bank%d" % (PACK + u if h == 0 else 2 + u % 2)) for u in range(PACK)]
-            for q in range(2):
-                for e in range(2):
-                    for t in range(PACK):
-                        nc.tensor.transpose(turned[2 * q + t // 2][:, t % 2, e * P : (e + 1) * P], act[:, 2 * q + e, t, :], ident[:])
+        def hidden(h, q, act, rounded, grouped):
+            turned = [psum.tile([P, 2, PART], F32, name="turned%d%d%d" % (h, q, u), tag="bank%d" % turn_banks[h][2 * q + u]) for u in range(2)]
+            for e in range(2):
                 for t in range(PACK):
-                    nc.scalar.activation(rounded[:, q, t, :], turned[2 * q + t // 2][:, t % 2, :], ACT.Copy, scale=sm_sb[:, t : t + 1])
-                interleave(grouped[:, q, :], rounded[:, q])
-            return grouped[:].rearrange("p q w -> p (q w)")
+                    nc.tensor.transpose(turned[t // 2][:, t % 2, e * P : (e + 1) * P], act[:, 2 * q + e, t, :], ident[:])
+            for t in range(PACK):
+                nc.scalar.activation(rounded[:, t, :], turned[t // 2][:, t % 2, :], ACT.Copy, scale=sm_sb[:, t : t + 1])
+            interleave(grouped, rounded)
 
-        def place(h, n, msg):
-            bank = psum.tile([P, HALF], F32, name="y%d%d" % (h, n), tag="bank%d" % (n % 2 if h == 0 else PACK + n))
-            wd_codes, wd_sc = wd_q[min(n, 1)]
-            cols = slice(max(n - 1, 0) * P, max(n, 1) * P)
+        def project(sums, n, h_codes, h_sc):
+            wd_codes, wd_sc = wd_q[n // 2]
+            cols = slice((n % 2) * P, (n % 2 + 1) * P)
             nc.tensor.matmul_mx(
-                out=bank[:],
+                out=sums,
                 lhsT=wd_codes[:, cols].bitcast(FP8X4),
                 lhsT_scale=wd_sc[:, cols],
-                rhs=h_q[h][0][:].bitcast(FP8X4),
-                rhs_scale=h_q[h][1][:],
+                rhs=h_codes.bitcast(FP8X4),
+                rhs_scale=h_sc,
                 start=True,
                 stop=True,
             )
-            nc.scalar.copy(msg[:], bank[:])
+
+        def scatter(n, msg, first, count):
             nc.vector.tensor_tensor(
-                windows[n][:].indirect(lists[1][:, h * COLS : (h + 1) * COLS]), msg[:], weighted[n][:, h * HALF : (h + 1) * HALF], MULT
+                windows[n][:].indirect(lists[1][:, first // 16 : (first + count) // 16]), msg, weighted[n][:, first : first + count], MULT
             )
+
+        def place(h, n, bank, msg):
+            sums = psum.tile([P, HALF], F32, name="y%d%d" % (h, n), tag="bank%d" % bank)
+            project(sums[:], n, h_q[h][0][:], h_q[h][1][:])
+            nc.scalar.copy(msg[:], sums[:])
+            scatter(n, msg[:], h * HALF, HALF)
+
+        def place_part(q, bank, msg):
+            edges = slice(q * PART, (q + 1) * PART)
+            sums = psum.tile([P, 2, PART], F32, name="y_part%d" % q, tag="bank%d" % bank)
+            for n in range(2):
+                project(sums[:, n, :], n, h_q[0][0][:, edges], h_q[0][1][:, edges])
+            nc.scalar.copy(msg[:], sums[:].rearrange("p n j -> p (n j)"))
+            for n in range(2):
+                scatter(n, msg[:, n * PART : (n + 1) * PART], q * PART, PART)
 
         def weigh(n, held):
             nc.vector.tensor_tensor(held[:], gates[n][:].indirect(lists[0][:]), wgo_sb[:], MULT)
             return held
 
         weighted = [weigh(n, sb("gate_w%d" % n, [P, J], F32)) for n in range(PAGES - 1)]
+        windows.append(at("window1", [P, T], F32, ws_raw0_at + LAP - PAGE_BYTES))
+        nc.gpsimd.memset(windows[1][:].bitcast(I32), 0)
         act = sb("act0", [P, PACK, PACK, P], F32)
-        wd_bf = [sb("wd_bf0", [P, P * PACK], BF16), at("wd_bf1", [P, REST * PACK], BF16, wd_bf1_at)]
         for b in range(PACK):
             activate(b, act[:, b])
-        interleave(wd_bf[0][:], wd_raw[0][:])
-        h_bf = hidden(0, act, at("rounded0", [P, 2, PACK, PART], BF16, rounded0_at), sb("h_bf0", [P, 2, PART * PACK], BF16))
-        wd_q = [quantise("wd0", wd_bf[0][:], P, rounded0_at)]
-        h_q = [quantise("h0", h_bf, HALF)]
-        weighted.append(weigh(PAGES - 1, at("gate_w3", [P, J], F32, rounded0_at + P * 4)))
-        interleave(wd_bf[1][:], wd_raw[1][:])
-        wd_q.append(quantise("wd1", wd_bf[1][:], REST))
-        for n, offset in ((1, wd_bf1_at + LAP - PAGE_BYTES), (2, wd_bf1_at + LAP)):
-            windows.append(at("window%d" % n, [P, T], F32, offset))
-            nc.gpsimd.memset(windows[n][:].bitcast(I32), 0)
-        place(0, 0, at("msg00", [P, HALF], F32, wd_raw1_at))
-        windows.append(at("window3", [P, T], F32, wd_raw1_at + LAP - PAGE_BYTES))
+        rounded = [sb("rounded00", [P, PACK, PART], BF16)[:], at("rounded01", [P, PACK, PART], BF16, rounded01_at)[:]]
+        h_bf = [sb("h_bf00", [P, PART * PACK], BF16)[:], at("h_bf01", [P, PART * PACK], BF16, window2_at)[:]]
+        wd_bf0 = sb("wd_bf0", [P, PART * PACK], BF16)
+        hidden(0, 0, act, rounded[0], h_bf[0])
+        interleave(wd_bf0[:], wd_raw[0][:])
+        hidden(0, 1, act, rounded[1], h_bf[1])
+        wd_q = [quantise("wd0", wd_bf0[:], PART)]
+        h_q = [(sb("h0_codes", [P, HALF], U32), at("h0_sc", [P, HALF], U8, wd_raw0_at))]
+
+        def quantise_part(q):
+            edges = slice(q * PART, (q + 1) * PART)
+            nc.vector.quantize_mx(out=h_q[0][0][:, edges].bitcast(FP8X4), scales=h_q[0][1][:, edges], in_=h_bf[q])
+
+        quantise_part(0)
+        weighted.append(weigh(PAGES - 1, sb("gate_w3", [P, J], F32)))
+        quantise_part(1)
+        windows.append(at("window2", [P, T], F32, window2_at))
+        nc.gpsimd.memset(windows[2][:].bitcast(I32), 0)
+        place_part(0, 0, at("msg_part0", [P, HALF], F32, wd_bf1_at - words))
+        wd_bf1 = at("wd_bf1", [P, PART * PACK], BF16, wd_bf1_at)
+        interleave(wd_bf1[:], wd_raw[1][:])
+        wd_q.append(quantise("wd1", wd_bf1[:], PART))
+        windows.append(at("window3", [P, T], F32, window3_at))
         nc.gpsimd.memset(windows[3][:].bitcast(I32), 0)
-        for n in (1, 2):
-            place(0, n, sb("msg0%d" % n, [P, HALF], F32))
-        act = at("act1", [P, PACK, PACK, P], F32, wd_raw1_at + words)
+        act = at("act1", [P, PACK, PACK, P], F32, act1_at)
         for b in range(PACK):
             activate(PACK + b, act[:, b])
-        h_bf = hidden(1, act, sb("rounded1", [P, 2, PACK, PART], BF16), sb("h_bf1", [P, 2, PART * PACK], BF16))
-        h_q.append(quantise("h1", h_bf, HALF))
-        place(0, 3, sb("msg03", [P, HALF], F32, tag="rounded1"))
-        for n in range(PAGES):
-            place(1, n, sb("msg1%d" % n, [P, HALF], F32))
+        place_part(1, 2, sb("msg_part1", [P, HALF], F32))
+        h_bf = sb("h_bf1", [P, 2, PART * PACK], BF16)
+        hidden(1, 0, act, sb("rounded10", [P, PACK, PART], BF16)[:], h_bf[:, 0, :])
+        place(0, 2, 5, sb("msg02", [P, HALF], F32, tag="rounded10"))
+        hidden(1, 1, act, sb("rounded11", [P, PACK, PART], BF16)[:], h_bf[:, 1, :])
+        h_q.append(quantise("h1", h_bf[:].rearrange("p q w -> p (q w)"), HALF))
+        place(0, 3, 4, sb("msg03", [P, HALF], F32, tag="rounded11"))
+        for n, bank in enumerate((3, 2, 6, 7)):
+            place(1, n, bank, sb("msg1%d" % n, [P, HALF], F32))
             nc.sync.dma_start(out[n * P : (n + 1) * P, :], windows[n][:])

@@ -27,7 +27,6 @@ COLS = HALF // 16
 PART = 2 * P
 LINE = 4
 PAGES = N // P
-WIDE = R // 2
 PAGE_BYTES = T * 4
 LAP = 64
 DEALT = J // P
@@ -91,8 +90,7 @@ def tile_list_msg_gelu_gate_kernel(
                 wt_sc[32 * q : 32 * q + 4, :].bitcast(I32).rearrange("p (a r) -> p a r", a=PASSES),
                 wt_scales[:, 4 * q : 4 * q + 4, :].bitcast(I32).rearrange("a p r -> p a r"),
             )
-        for c in range(2):
-            nc.sync.dma_start(ws_raw[1][:, :, c * WIDE : (c + 1) * WIDE], ws_rows[1][:, :, c * WIDE : (c + 1) * WIDE])
+        nc.sync.dma_start(ws_raw[1][:], ws_rows[1])
 
         picked_sc = sb("picked_sc", [P, 2 * J], U8)
         for side in range(2):
@@ -132,9 +130,8 @@ def tile_list_msg_gelu_gate_kernel(
             )
 
         ws_bf = [at("ws_bf0", [P, R * PACK], BF16, ws_bf0_at), at("ws_bf1", [P, R * PACK], BF16, ws_bf1_at)]
-        interleave(ws_bf[0][:], ws_raw[0][:])
-        for c in range(2):
-            interleave(ws_bf[1][:, c * WIDE * PACK : (c + 1) * WIDE * PACK], ws_raw[1][:, :, c * WIDE : (c + 1) * WIDE])
+        for a in range(PASSES):
+            interleave(ws_bf[a][:], ws_raw[a][:])
 
         wt_codes = at("wt_codes", [P, PASSES, R], I32, wt_codes_at)
         nc.sync.dma_start(wt_codes[:], wt_words.rearrange("a p r b -> p a (r b)").bitcast(I32))

@@ -29,6 +29,7 @@ LINE = 4
 PAGES = N // P
 PAGE_BYTES = T * 4
 LAP = 64
+RUN = 32
 DEALT = J // P
 
 
@@ -115,8 +116,8 @@ def tile_list_msg_gelu_gate_kernel(
 
         def part_words(parted, picked):
             nc.vector.tensor_copy(
-                parted[:].bitcast(U16).rearrange("p (a j) -> p a j", a=PASSES),
-                picked[:].bitcast(U16).rearrange("p (j a) -> p a j", a=PASSES),
+                parted[:].bitcast(U16).rearrange("p (a r g j) -> p g r a j", a=PASSES, g=2, j=RUN),
+                picked[:].bitcast(U16).rearrange("p (r g j a) -> p g r a j", a=PASSES, g=2, j=RUN),
             )
 
         wgo_sb = sb("wgo_sb", [P, J], F32)

from contextlib import ExitStack

import concourse.mybir as mybir
from concourse.masks import make_identity

K, R, N, T, J = 1024, 512, 512, 2048, 1024
FLOPS = 2 * J * R * (2 * K + N)

F32 = mybir.dt.float32
BF16 = mybir.dt.bfloat16
I32 = mybir.dt.int32
U32 = mybir.dt.uint32
U16 = mybir.dt.uint16
U8 = mybir.dt.uint8
FP8X4 = mybir.dt.float8_e4m3fn_x4
FP4X4 = mybir.dt.float4_e2m1fn_x4
MULT = mybir.AluOpType.mult
ACT = mybir.ActivationFunctionType

P = 128
PACK = 4
PASSES = K // (P * PACK)
QUADS = 4
HALF = 512
HALVES = J // HALF
COLS = HALF // 16
PART = 2 * P
LINE = 4
PAGES = N // P
PAGE_BYTES = T * 4
LAP = 64
RUN = 32
DEALT = J // P


def tile_list_msg_gelu_gate_kernel(
    tc, tab_words, tab_scales, ws, wt_words, wt_scales, sm, wd, gT, wgo, offs, offs2, out
):
    nc = tc.nc
    with ExitStack() as ctx:
        keep = ctx.enter_context(tc.tile_pool(name="keep", bufs=1))
        laid = ctx.enter_context(tc.tile_pool(name="laid", bufs=1))
        psum = ctx.enter_context(tc.psum_pool(name="psum", bufs=1))

        def sb(name, shape, dtype, tag=None):
            return keep.tile(shape, dtype, name=name, tag=tag or name, align_bytes=64)

        def at(name, shape, dtype, offset):
            return laid.tile(shape, dtype, name=name, tag=name, align_bytes=64, offset=offset)

        words = HALF * 4
        wt_codes_at = 0
        tab_sc_at = wt_codes_at + PASSES * R * 4 - LAP
        ws_raw0_at = tab_sc_at + T + PAGE_BYTES - LAP
        wd_raw1_at = ws_raw0_at + LAP + 2 * words
        act1_at = wd_raw1_at + words
        ws_bf0_at = act1_at + 2 * PAGE_BYTES - LAP
        gates2_at = ws_bf0_at + LAP
        ws_bf1_at = gates2_at + 2 * PAGE_BYTES - LAP
        wd_raw0_at = ws_bf1_at + LAP
        wd_bf1_at = wd_raw0_at + 2 * words
        rounded01_at = wd_bf1_at - LAP
        window3_at = wd_bf1_at + words - LAP
        ws_raw1_at = window3_at + PAGE_BYTES
        window2_at = ws_raw1_at + 2 * words + PAGE_BYTES

        lists = [keep.tile([P, J // 16], U16, name="src_list"), keep.tile([P, J // 16], U16, name="dst_list")]
        tab_sc = at("tab_sc", [P, T], U8, tab_sc_at)
        wt_sc = sb("wt_sc", [P, PASSES * R], U8)
        tab_planes = sb("tab_planes", [P, PASSES * 2 * J], U8)
        ident = sb("ident", [P, P], F32)

        make_identity(nc, ident[:])
        nc.vector.memset(wt_sc[:].bitcast(I32), 0)
        nc.vector.memset(tab_sc[0:96, :].bitcast(I32), 0)
        nc.vector.memset(tab_planes[:].bitcast(I32), 0)

        nc.sync.dma_start(lists[0][:], offs)
        nc.scalar.dma_start(tab_sc[96:P, :].bitcast(I32), tab_scales.rearrange("a q t -> q a t").bitcast(I32))
        nc.sync.dma_start(lists[1][:], offs2)
        wgo_dealt = sb("wgo_dealt", [P, DEALT], F32)
        nc.scalar.dma_start(wgo_dealt[:], wgo[0].rearrange("(p m) -> p m", m=DEALT))

        ws_raw = [at("ws_raw0", [P, PACK, R], F32, ws_raw0_at), at("ws_raw1", [P, PACK, R], F32, ws_raw1_at)]
        ws_rows = ws.rearrange("(a p i) r -> a p i r", a=PASSES, i=PACK)
        tab_w = sb("tab_w", [P, T], I32)
        nc.sync.dma_start(ws_raw[0][:], ws_rows[0])
        nc.sync.dma_start(tab_w[:], tab_words[0].rearrange("p t b -> p (t b)").bitcast(I32))
        for q in range(QUADS):
            nc.sync.dma_start(
                wt_sc[32 * q : 32 * q + 4, :].bitcast(I32).rearrange("p (a r) -> p a r", a=PASSES),
                wt_scales[:, 4 * q : 4 * q + 4, :].bitcast(I32).rearrange("a p r -> p a r"),
            )
        nc.sync.dma_start(ws_raw[1][:], ws_rows[1])

        picked_sc = sb("picked_sc", [P, 2 * J], U8)
        for side in range(2):
            nc.vector.tensor_copy(picked_sc[:, side * J : (side + 1) * J], tab_sc[:].indirect(lists[side][:]))
        for q in range(QUADS):
            nc.sync.dma_start(
                tab_planes[32 * q : 32 * q + 4, :].bitcast(I32).rearrange("p (a j) -> p a j", a=PASSES),
                picked_sc[96 + 8 * q : 96 + 8 * q + 8, :].bitcast(I32),
            )

        def interleave(grouped, planes):
            nc.scalar.copy(grouped.rearrange("p (j c t) -> p j t c", t=PACK, c=LINE), planes.rearrange("p t (j c) -> p j t c", c=LINE))

        def quantise(name, grouped, width):
            codes = sb(name + "_codes", [P, width], U32)
            scales = sb(name + "_sc", [P, width], U8)
            nc.vector.quantize_mx(out=codes[:].bitcast(FP8X4), scales=scales[:], in_=grouped)
            return codes, scales

        def pick_words(picked, h, side):
            nc.vector.tensor_copy(picked[:], tab_w[:].bitcast(U32).indirect(lists[side][:, h * COLS : (h + 1) * COLS]))

        def part_words(parted, picked):
            nc.vector.tensor_copy(
                parted[:].bitcast(U16).rearrange("p (a r g j) -> p g r a j", a=PASSES, g=2, j=RUN),
                picked[:].bitcast(U16).rearrange("p (r g j a) -> p g r a j", a=PASSES, g=2, j=RUN),
            )

        wgo_sb = sb("wgo_sb", [P, J], F32)
        for u in range(DEALT // LINE):
            spread = psum.tile([P, LINE, P], F32, name="spread%d" % u, tag="bank%d" % u)
            for m in range(LINE):
                column = wgo_dealt[:, LINE * u + m : LINE * u + m + 1]
                nc.tensor.transpose(spread[:, m, :], column.to_broadcast([P, P]), ident[:])
            nc.scalar.copy(
                wgo_sb[:].rearrange("p (n m) -> p n m", m=DEALT)[:, :, LINE * u : LINE * (u + 1)], spread[:].rearrange("p m n -> p n m")
            )

        ws_bf = [at("ws_bf0", [P, R * PACK], BF16, ws_bf0_at), at("ws_bf1", [P, R * PACK], BF16, ws_bf1_at)]
        for a in range(PASSES):
            interleave(ws_bf[a][:], ws_raw[a][:])

        wt_codes = at("wt_codes", [P, PASSES, R], I32, wt_codes_at)
        nc.sync.dma_start(wt_codes[:], wt_words.rearrange("a p r b -> p a (r b)").bitcast(I32))
        sm_sb = at("sm_sb", [P, PACK], F32, tab_sc_at + LAP)
        gates = {
            0: at("gates0", [P, T], F32, ws_raw0_at + LAP - PAGE_BYTES),
            1: at("gates1", [P, T], F32, gates2_at - PAGE_BYTES),
            2: at("gates2", [P, T], F32, gates2_at),
            3: at("gates3", [P, T], F32, ws_bf1_at + LAP - PAGE_BYTES),
        }
        wd_raw = [at("wd_raw%d" % c, [P, PACK, PART], F32, offset) for c, offset in enumerate((wd_raw0_at, wd_raw1_at))]
        wd_rows = wd.rearrange("(p t) n -> p t n", t=PACK)
        nc.sync.dma_start(sm_sb[:], sm.rearrange("(p t) -> p t", t=PACK))
        for n in range(PAGES - 1):
            nc.sync.dma_start(gates[n][:], gT[n * P : (n + 1) * P, :])
        nc.sync.dma_start(wd_raw[0][:], wd_rows[:, :, 0:PART])
        nc.sync.dma_start(gates[PAGES - 1][:], gT[N - P : N, :])

        picked = [
            [sb("picked00", [P, HALF], U32), at("picked01", [P, HALF], U32, ws_raw0_at + LAP)],
            [at("picked10", [P, HALF], U32, ws_raw0_at + LAP + 2 * words), at("picked11", [P, HALF], U32, ws_raw1_at + 2 * words)],
        ]
        parted = [
            [at("parted00", [P, words], U8, ws_raw0_at + LAP + words), sb("parted01", [P, words], U8)],
            [at("parted10", [P, words], U8, ws_raw1_at + words), sb("parted11", [P, words], U8)],
        ]
        ws_q = []
        pick_words(picked[0][0], 0, 0)
        ws_q.append(quantise("ws0", ws_bf[0][:], R))
        part_words(parted[0][0], picked[0][0])
        pick_words(picked[0][1], 0, 1)
        pick_words(picked[1][0], 1, 0)
        part_words(parted[0][1], picked[0][1])
        ws_q.append(quantise("ws1", ws_bf[1][:], R))
        pick_words(picked[1][1], 1, 1)
        for side in range(2):
            part_words(parted[1][side], picked[1][side])
        nc.sync.dma_start(wd_raw[1][:], wd_rows[:, :, PART:N])
        windows = [at("window0", [P, T], F32, ws_raw1_at + 2 * words)]
        nc.gpsimd.memset(windows[0][:].bitcast(I32), 0)
        sum_banks = (0, 1, 2, 3, 2, 3, 4, 5)
        turn_banks = ((4, 5, 6, 7), (6, 7, 6, 7))

        def activate(b, act):
            h, first = divmod(b * P, HALF)
            bank = psum.tile([P, R], F32, name="sum%d" % b, tag="bank%d" % sum_banks[b])
            order = [(0, 0), (1, 0), (1, 1), (0, 1)]
            for step, (side, a) in enumerate(order):
                if side == 0:
                    w_codes, w_sc = ws_q[a][0][:], ws_q[a][1][:]
                else:
                    w_codes, w_sc = wt_codes[:, a, :], wt_sc[:, a * R : (a + 1) * R]
                word = a * HALF + first
                edge = (2 * a + side) * J + b * P
                nc.tensor.matmul_mx(
                    out=bank[:],
                    lhsT=parted[h][side][:, 2 * word : 2 * (word + P)].bitcast(FP4X4),
                    lhsT_scale=tab_planes[:, edge : edge + P],
                    rhs=w_codes.bitcast(FP8X4),
                    rhs_scale=w_sc,
                    start=(step == 0),
                    stop=(step == len(order) - 1),
                )
            nc.scalar.activation(act, bank[:].rearrange("p (m t) -> p t m", t=PACK), ACT.Gelu_apprx_tanh)

        def hidden(h, q, act, rounded, grouped):
            turned = [psum.tile([P, 2, PART], F32, name="turned%d%d%d" % (h, q, u), tag="bank%d" % turn_banks[h][2 * q + u]) for u in range(2)]
            for e in range(2):
                for t in range(PACK):
                    nc.tensor.transpose(turned[t // 2][:, t % 2, e * P : (e + 1) * P], act[:, 2 * q + e, t, :], ident[:])
            for t in range(PACK):
                nc.scalar.activation(rounded[:, t, :], turned[t // 2][:, t % 2, :], ACT.Copy, scale=sm_sb[:, t : t + 1])
            interleave(grouped, rounded)

        def project(sums, n, h_codes, h_sc):
            wd_codes, wd_sc = wd_q[n // 2]
            cols = slice((n % 2) * P, (n % 2 + 1) * P)
            nc.tensor.matmul_mx(
                out=sums,
                lhsT=wd_codes[:, cols].bitcast(FP8X4),
                lhsT_scale=wd_sc[:, cols],
                rhs=h_codes.bitcast(FP8X4),
                rhs_scale=h_sc,
                start=True,
                stop=True,
            )

        def scatter(n, msg, first, count):
            nc.vector.tensor_tensor(
                windows[n][:].indirect(lists[1][:, first // 16 : (first + count) // 16]), msg, weighted[n][:, first : first + count], MULT
            )

        def place(h, n, bank, msg):
            sums = psum.tile([P, HALF], F32, name="y%d%d" % (h, n), tag="bank%d" % bank)
            project(sums[:], n, h_q[h][0][:], h_q[h][1][:])
            nc.scalar.copy(msg[:], sums[:])
            scatter(n, msg[:], h * HALF, HALF)

        def place_part(q, bank, msg):
            edges = slice(q * PART, (q + 1) * PART)
            sums = psum.tile([P, 2, PART], F32, name="y_part%d" % q, tag="bank%d" % bank)
            for n in range(2):
                project(sums[:, n, :], n, h_q[0][0][:, edges], h_q[0][1][:, edges])
            nc.scalar.copy(msg[:], sums[:].rearrange("p n j -> p (n j)"))
            for n in range(2):
                scatter(n, msg[:, n * PART : (n + 1) * PART], q * PART, PART)

        def weigh(n, held):
            nc.vector.tensor_tensor(held[:], gates[n][:].indirect(lists[0][:]), wgo_sb[:], MULT)
            return held

        weighted = [weigh(n, sb("gate_w%d" % n, [P, J], F32)) for n in range(PAGES - 1)]
        windows.append(at("window1", [P, T], F32, ws_raw0_at + LAP - PAGE_BYTES))
        nc.gpsimd.memset(windows[1][:].bitcast(I32), 0)
        act = sb("act0", [P, PACK, PACK, P], F32)
        for b in range(PACK):
            activate(b, act[:, b])
        rounded = [sb("rounded00", [P, PACK, PART], BF16)[:], at("rounded01", [P, PACK, PART], BF16, rounded01_at)[:]]
        h_bf = [sb("h_bf00", [P, PART * PACK], BF16)[:], at("h_bf01", [P, PART * PACK], BF16, window2_at)[:]]
        wd_bf0 = sb("wd_bf0", [P, PART * PACK], BF16)
        hidden(0, 0, act, rounded[0], h_bf[0])
        interleave(wd_bf0[:], wd_raw[0][:])
        hidden(0, 1, act, rounded[1], h_bf[1])
        wd_q = [quantise("wd0", wd_bf0[:], PART)]
        h_q = [(sb("h0_codes", [P, HALF], U32), at("h0_sc", [P, HALF], U8, wd_raw0_at))]

        def quantise_part(q):
            edges = slice(q * PART, (q + 1) * PART)
            nc.vector.quantize_mx(out=h_q[0][0][:, edges].bitcast(FP8X4), scales=h_q[0][1][:, edges], in_=h_bf[q])

        quantise_part(0)
        weighted.append(weigh(PAGES - 1, sb("gate_w3", [P, J], F32)))
        quantise_part(1)
        windows.append(at("window2", [P, T], F32, window2_at))
        nc.gpsimd.memset(windows[2][:].bitcast(I32), 0)
        place_part(0, 0, at("msg_part0", [P, HALF], F32, wd_bf1_at - words))
        wd_bf1 = at("wd_bf1", [P, PART * PACK], BF16, wd_bf1_at)
        interleave(wd_bf1[:], wd_raw[1][:])
        wd_q.append(quantise("wd1", wd_bf1[:], PART))
        windows.append(at("window3", [P, T], F32, window3_at))
        nc.gpsimd.memset(windows[3][:].bitcast(I32), 0)
        act = at("act1", [P, PACK, PACK, P], F32, act1_at)
        for b in range(PACK):
            activate(PACK + b, act[:, b])
        place_part(1, 2, sb("msg_part1", [P, HALF], F32))
        h_bf = sb("h_bf1", [P, 2, PART * PACK], BF16)
        hidden(1, 0, act, sb("rounded10", [P, PACK, PART], BF16)[:], h_bf[:, 0, :])
        place(0, 2, 5, sb("msg02", [P, HALF], F32, tag="rounded10"))
        hidden(1, 1, act, sb("rounded11", [P, PACK, PART], BF16)[:], h_bf[:, 1, :])
        h_q.append(quantise("h1", h_bf[:].rearrange("p q w -> p (q w)"), HALF))
        place(0, 3, 4, sb("msg03", [P, HALF], F32, tag="rounded11"))
        for n, bank in enumerate((3, 2, 6, 7)):
            place(1, n, bank, sb("msg1%d" % n, [P, HALF], F32))
            nc.sync.dma_start(out[n * P : (n + 1) * P, :], windows[n][:])
